import numpy as np
import ml_dtypes


def mxq(x, axis, fmt="e4m3"):
    dtype, down = {"e4m3": (ml_dtypes.float8_e4m3fn, 7), "e5m2": (ml_dtypes.float8_e5m2, 14)}[fmt]
    v = np.moveaxis(np.asarray(x, np.float32).astype(ml_dtypes.bfloat16).astype(np.float64), axis, -1)
    blocks = v.reshape(v.shape[:-1] + (-1, 32))
    amax = np.abs(blocks).max(-1, keepdims=True)
    byte = np.maximum(np.where(amax > 0, np.frexp(amax)[1] - 1 + 127, 0) - down, 1)
    scale = np.exp2(byte - 127.0)
    codes = (blocks / scale).astype(np.float32).astype(dtype).astype(np.float64)
    return np.moveaxis((codes * scale).reshape(v.shape), -1, axis)


WIDE = False


def mx_kscale(k):
    if not WIDE:
        return np.ones(k)
    levels = np.array([24, -24, 12, -12, 0])
    if k % 512:
        return np.exp2(np.random.permutation(np.resize(levels, k // 32))).repeat(32)
    a = np.empty((k // 512, 16))
    for p in range(k // 512):
        a[p, :8] = np.random.permutation(np.resize(levels, 8))
        for g in range(8):
            far = levels[np.abs(levels - a[p, g]) >= 10]
            a[p, g + 8] = far[np.random.randint(len(far))]
    return np.exp2(a.ravel()).repeat(32)


def f64(x):
    return np.asarray(x).astype(np.float64)


def striped(idx):
    return np.tile(idx.reshape(-1, 16).T, (8, 1)).astype(np.uint16)


def unstriped(offs):
    return offs[:16].T.reshape(-1).astype(np.int64)


E2M1 = np.array([0.0, 0.5, 1.0, 1.5, 2.0, 3.0, 4.0, 6.0, -0.0, -0.5, -1.0, -1.5, -2.0, -3.0, -4.0, -6.0])


def pack_weight(w, fmt):
    k, n = w.shape
    w = f64(np.asarray(w, np.float32).astype(ml_dtypes.bfloat16)).reshape(k // 32, 32, n)
    amax = np.abs(w).max(1)
    if fmt == "e4m3":
        byte = np.frexp(amax)[1] - 1 + 127 - 7
    else:
        mant, ex = np.frexp(amax / 6.0)
        byte = np.where(mant > 0.5, ex, ex - 1) + 127
    byte = np.clip(np.where(amax > 0, byte, 1), 1, 254)
    scaled = (w * np.exp2(127.0 - byte)[:, None, :]).reshape(k, n).astype(np.float32)
    by_word = np.ascontiguousarray(scaled.reshape(k // 512, 128, 4, n).transpose(0, 1, 3, 2))
    if fmt == "e4m3":
        words = by_word.astype(ml_dtypes.float8_e4m3fn).view(np.uint8)
    else:
        c = by_word.astype(ml_dtypes.float4_e2m1fn).view(np.uint8) & 0xF
        words = (c[..., 0::2] | (c[..., 1::2] << 4)).reshape(k // 512, 128, 2 * n)
    return np.ascontiguousarray(words), np.ascontiguousarray(byte.astype(np.uint8).reshape(k // 512, 16, n))


def unpack_weight(words, scales, fmt):
    g, _, n = scales.shape
    words = np.ascontiguousarray(words).reshape(g, 128, n, -1)
    if fmt == "e4m3":
        vals = words.view(ml_dtypes.float8_e4m3fn).astype(np.float64)
    else:
        nib = np.empty((g, 128, n, 4), np.uint8)
        nib[..., 0::2] = words & 0xF
        nib[..., 1::2] = words >> 4
        vals = E2M1[nib]
    vals = vals * np.repeat(np.exp2(scales.astype(np.float64) - 127.0), 8, axis=1)[..., None]
    return vals.transpose(0, 1, 3, 2).reshape(g * 512, n)


def planes(y):
    n, m = y.shape
    v = y.astype(np.float32).astype(ml_dtypes.bfloat16).astype(np.float64).reshape(n // 32, 32, m)
    top = np.abs(v).max(1)
    byte = np.clip(np.where(top > 0, np.frexp(top)[1] - 1 + 127 - 7, 1), 1, 254)
    codes = (v * np.exp2(127.0 - byte)[:, None, :]).reshape(n, m).astype(np.float32).astype(ml_dtypes.float8_e4m3fn).view(np.uint8)
    words = codes.reshape(n // 512, 128, 4, m).transpose(0, 1, 3, 2)
    return np.ascontiguousarray(words), np.ascontiguousarray(byte.astype(np.uint8).reshape(n // 512, 16, m))


def sigm(f):
    return 1.0 / (1.0 + np.exp(-np.maximum(f, -700.0)))


K, N, T, J = 512, 512, 4096, 1024


def setup_inputs():
    n = np.random.standard_normal
    s = mx_kscale(K)[:, None]
    p_tab = pack_weight(n((K, T)) * s, "e4m3")
    p_wv4 = pack_weight(n((K, N)) / np.sqrt(K) / s, "e2m1")
    return {
        "tab_words": p_tab[0],
        "tab_scales": p_tab[1],
        "wk": (n((K, N)) / np.sqrt(K) / s).astype(np.float32),
        "wv4_words": p_wv4[0],
        "wv4_scales": p_wv4[1],
        "wvd": (0.4 * (n((K, N)) / np.sqrt(K) / s)).astype(np.float32),
        "st": (n((N, J))).astype(np.float32),
        "rT": (n((N, T))).astype(np.float32),
        "offs": striped(np.random.permutation(T)[:J]),
    }


def reference(tab_words, tab_scales, wk, wv4_words, wv4_scales, wvd, st, rT, offs):
    idx = unstriped(offs)
    tab_ = unpack_weight(tab_words, tab_scales, "e4m3")[:, idx]
    wk_ = mxq(f64(wk), 0, "e4m3")
    wv4_ = unpack_weight(wv4_words, wv4_scales, "e2m1")
    wvd_ = mxq(f64(wvd), 0, "e4m3")
    ke = wk_.T @ tab_
    ve = wv4_.T @ tab_ + wvd_.T @ tab_
    gate = sigm(ke * f64(st))
    out_0 = f64(rT)[:, idx] + gate * ve
    return (out_0,) + planes(out_0)

@@ -1,0 +1,179 @@
+from contextlib import ExitStack
+
+import concourse.mybir as mybir
+
+K, N, T, J = 512, 512, 4096, 1024
+FLOPS = 3 * 2 * K * N * J
+
+F32 = mybir.dt.float32
+BF16 = mybir.dt.bfloat16
+I32 = mybir.dt.int32
+U32 = mybir.dt.uint32
+U16 = mybir.dt.uint16
+U8 = mybir.dt.uint8
+FP8X4 = mybir.dt.float8_e4m3fn_x4
+FP4X4 = mybir.dt.float4_e2m1fn_x4
+MULT = mybir.AluOpType.mult
+ADD = mybir.AluOpType.add
+SIGMOID = mybir.ActivationFunctionType.Sigmoid
+
+P = 128
+PACK = 4
+HALF = 512
+CHUNKS = [(0, 256), (256, 512), (512, 768), (768, 1024)]
+
+
+def load_scale_rows(queue, plane, rows):
+    for q in range(4):
+        queue.dma_start(out=plane[32 * q : 32 * q + 4, :].bitcast(I32), in_=rows[0, 4 * q : 4 * q + 4, :].bitcast(I32))
+
+
+def tile_list_engram_dl_sigLP_kernel(
+    tc, tab_words, tab_scales, wk, wv4_words, wv4_scales, wvd, st, rT, offs, out_0, out_1, out_2
+):
+    nc = tc.nc
+    with ExitStack() as ctx:
+        keep = ctx.enter_context(tc.tile_pool(name="keep", bufs=1))
+        ring = ctx.enter_context(tc.tile_pool(name="ring", bufs=3))
+        psum = ctx.enter_context(tc.psum_pool(name="psum", bufs=4))
+
+        offsets = keep.tile([P, J // 16], U16, name="offsets")
+        tw = keep.tile([P, T], U32, name="tw", align_bytes=64)
+        ts = keep.tile([P, T], U8, name="ts", align_bytes=64)
+        wk_raw = keep.tile([P, PACK, N], F32, name="wk_raw")
+        wd_raw = keep.tile([P, PACK, N], F32, name="wd_raw")
+        w4_raw = keep.tile([P, 2 * N], U8, name="w4_raw", align_bytes=64)
+        s4_raw = keep.tile([P, N], U8, name="s4_raw", align_bytes=64)
+        st_sb = [keep.tile([P, J], F32, name="st%d" % t) for t in range(PACK)]
+        r_sb = [keep.tile([P, T], F32, name="r%d" % t) for t in range(PACK)]
+
+        nc.vector.memset(ts[:].bitcast(I32), 0)
+        nc.vector.memset(s4_raw[:].bitcast(I32), 0)
+
+        st_rows = st.rearrange("(p t) j -> p t j", t=PACK)
+        r_rows = rT.rearrange("(p t) c -> p t c", t=PACK)
+        y_rows = out_0.rearrange("(p t) j -> p t j", t=PACK)
+
+        nc.sync.dma_start(offsets[:], offs)
+        nc.sync.dma_start(out=wk_raw[:], in_=wk.rearrange("(p i) n -> p i n", i=PACK))
+        load_scale_rows(nc.sync, ts, tab_scales)
+        nc.sync.dma_start(out=w4_raw[:].bitcast(I32), in_=wv4_words[0].bitcast(I32))
+        nc.sync.dma_start(out=tw[:].bitcast(I32), in_=tab_words[0].rearrange("p t i -> p (t i)").bitcast(I32))
+        load_scale_rows(nc.sync, s4_raw, wv4_scales)
+        nc.sync.dma_start(out=st_sb[0][:], in_=st_rows[:, 0, :])
+        nc.sync.dma_start(out=wd_raw[:], in_=wvd.rearrange("(p i) n -> p i n", i=PACK))
+        for t in range(1, PACK):
+            nc.sync.dma_start(out=st_sb[t][:], in_=st_rows[:, t, :])
+        for t in range(PACK):
+            nc.sync.dma_start(out=r_sb[t][:], in_=r_rows[:, t, :])
+
+        def round_weight(raw, name):
+            grouped = keep.tile([P, PACK, P, PACK], BF16, name=name, align_bytes=64)
+            nc.scalar.copy(
+                out=grouped[:].rearrange("p t m i -> p m i t"),
+                in_=raw[:].rearrange("p i (m t) -> p m i t", t=PACK),
+            )
+            return grouped
+
+        def quantise_weight(grouped, name):
+            codes = keep.tile([P, N], U32, name=name + "_codes", align_bytes=64)
+            scales = keep.tile([P, N], U8, name=name + "_scales", align_bytes=64)
+            nc.vector.quantize_mx(
+                out=codes[:].bitcast(FP8X4), scales=scales[:], in_=grouped[:].rearrange("p t m i -> p (t m i)")
+            )
+            return codes, scales
+
+        wk_grouped = round_weight(wk_raw, "wk_grouped")
+
+        gs = keep.tile([P, J], U8, name="gs", align_bytes=64)
+        nc.vector.tensor_copy(gs[:], ts[:].indirect(offsets[:]))
+
+        w4 = keep.tile([P, 2 * N], U8, name="w4", align_bytes=64)
+        s4 = keep.tile([P, N], U8, name="s4", align_bytes=64)
+        nc.vector.tensor_copy(
+            out=w4[:].rearrange("p (t m b) -> p m t b", t=PACK, b=2),
+            in_=w4_raw[:].rearrange("p (m t b) -> p m t b", t=PACK, b=2),
+        )
+        wk_codes, wk_scales = quantise_weight(wk_grouped, "wk")
+
+        gw = [keep.tile([P, HALF], U32, name="gw%d" % h, align_bytes=64) for h in range(2)]
+        for h in range(2):
+            nc.vector.tensor_copy(gw[h][:], tw[:].indirect(offsets[:, h * HALF // 16 : (h + 1) * HALF // 16]))
+
+        nc.vector.tensor_copy(
+            out=s4[:].rearrange("p (t m) -> p m t", t=PACK),
+            in_=s4_raw[:].rearrange("p (m t) -> p m t", t=PACK),
+        )
+        wd_grouped = round_weight(wd_raw, "wd_grouped")
+        wd_codes, wd_scales = quantise_weight(wd_grouped, "wd")
+
+        gv = [keep.tile([P, J], F32, name="gv%d" % t) for t in range(PACK)]
+        units = [(t, h) for t in range(PACK) for h in range(2)]
+        gates = {}
+
+        def make_gate(t, h):
+            cols = slice(h * HALF, (h + 1) * HALF)
+            ms = slice(t * P, (t + 1) * P)
+            ke = psum.tile([P, HALF], F32, name="ke")
+            nc.tensor.matmul_mx(
+                out=ke[:], lhsT=wk_codes[:, ms].bitcast(FP8X4), lhsT_scale=wk_scales[:, ms],
+                rhs=gw[h][:].bitcast(FP8X4), rhs_scale=gs[:, cols], start=True, stop=True,
+            )
+            z = ring.tile([P, HALF], F32, name="z")
+            nc.vector.tensor_tensor(z[:], ke[:], st_sb[t][:, cols], MULT)
+            gate = ring.tile([P, HALF], F32, name="gate")
+            nc.scalar.activation(gate[:], z[:], SIGMOID)
+            gates[(t, h)] = gate
+
+        def make_value(t, h):
+            cols = slice(h * HALF, (h + 1) * HALF)
+            ms = slice(t * P, (t + 1) * P)
+            ve = psum.tile([P, HALF], F32, name="ve")
+            nc.tensor.matmul_mx(
+                out=ve[:], lhsT=w4[:, 2 * t * P : 2 * (t + 1) * P].bitcast(FP4X4), lhsT_scale=s4[:, ms],
+                rhs=gw[h][:].bitcast(FP8X4), rhs_scale=gs[:, cols], start=True, stop=False,
+            )
+            nc.tensor.matmul_mx(
+                out=ve[:], lhsT=wd_codes[:, ms].bitcast(FP8X4), lhsT_scale=wd_scales[:, ms],
+                rhs=gw[h][:].bitcast(FP8X4), rhs_scale=gs[:, cols], start=False, stop=True,
+            )
+            nc.vector.tensor_tensor(gv[t][:, cols], ve[:], gates[(t, h)][:], MULT)
+
+        make_gate(*units[0])
+        make_gate(*units[1])
+        for u in range(len(units)):
+            if u + 2 < len(units):
+                make_gate(*units[u + 2])
+            make_value(*units[u])
+
+        y01 = keep.tile([P, 2, J], F32, name="y01")
+        for t in range(2):
+            nc.vector.tensor_tensor(y01[:, t, :], r_sb[t][:].indirect(offsets[:]), gv[t][:], ADD)
+        nc.sync.dma_start(out=y_rows[:, 0:2, :], in_=y01[:])
+
+        yb = [keep.tile([P, b - a, PACK], BF16, name="yb%d" % a, align_bytes=64) for a, b in CHUNKS]
+        y23 = [keep.tile([P, 2, b - a], F32, name="y23_%d" % a) for a, b in CHUNKS]
+        for c, (a, b) in enumerate(CHUNKS):
+            nc.scalar.copy(out=yb[c][:, :, 0:2], in_=y01[:, :, a:b].rearrange("p t j -> p j t"))
+        for t in range(2, PACK):
+            for c, (a, b) in enumerate(CHUNKS):
+                nc.vector.tensor_tensor(
+                    y23[c][:, t - 2, :], r_sb[t][:].indirect(offsets[:, a // 16 : b // 16]), gv[t][:, a:b], ADD
+                )
+        for c, (a, b) in enumerate(CHUNKS):
+            nc.scalar.copy(out=yb[c][:, :, 2:4], in_=y23[c][:].rearrange("p t j -> p j t"))
+            nc.sync.dma_start(out=y_rows[:, 2:4, a:b], in_=y23[c][:])
+
+        y_codes = keep.tile([P, J], U32, name="y_codes", align_bytes=64)
+        y_scales = keep.tile([P, J], U8, name="y_scales", align_bytes=64)
+        word_rows = out_1[0].rearrange("p j i -> p (j i)").bitcast(I32)
+        for c, (a, b) in enumerate(CHUNKS):
+            nc.vector.quantize_mx(
+                out=y_codes[:, a:b].bitcast(FP8X4), scales=y_scales[:, a:b], in_=yb[c][:].rearrange("p j t -> p (j t)")
+            )
+            nc.sync.dma_start(out=word_rows[:, a:b], in_=y_codes[:, a:b].bitcast(I32))
+        for q in range(4):
+            queue = nc.sync if q % 2 == 0 else nc.scalar
+            queue.dma_start(
+                out=out_2[0, 4 * q : 4 * q + 4, :].bitcast(I32), in_=y_scales[32 * q : 32 * q + 4, :].bitcast(I32)
+            )

@@ -20,12 +20,12 @@ SIGMOID = mybir.ActivationFunctionType.Sigmoid
 P = 128
 PACK = 4
 HALF = 512
-CHUNKS = [(0, 256), (256, 512), (512, 768), (768, 1024)]
+CHUNKS = [(0, 128), (128, 384), (384, 640), (640, 896), (896, 1024)]
 
 
 def load_scale_rows(queue, plane, rows):
-    for q in range(4):
-        queue.dma_start(out=plane[32 * q : 32 * q + 4, :].bitcast(I32), in_=rows[0, 4 * q : 4 * q + 4, :].bitcast(I32))
+    for r in range(4):
+        queue.dma_start(out=plane[r:P:32, :].bitcast(I32), in_=rows[0, r:16:4, :].bitcast(I32))
 
 
 def tile_list_engram_dl_sigLP_kernel(
@@ -34,7 +34,7 @@ def tile_list_engram_dl_sigLP_kernel(
     nc = tc.nc
     with ExitStack() as ctx:
         keep = ctx.enter_context(tc.tile_pool(name="keep", bufs=1))
-        ring = ctx.enter_context(tc.tile_pool(name="ring", bufs=3))
+        ring = ctx.enter_context(tc.tile_pool(name="ring", bufs=8))
         psum = ctx.enter_context(tc.psum_pool(name="psum", bufs=4))
 
         offsets = keep.tile([P, J // 16], U16, name="offsets")
@@ -47,22 +47,29 @@ def tile_list_engram_dl_sigLP_kernel(
         st_sb = [keep.tile([P, J], F32, name="st%d" % t) for t in range(PACK)]
         r_sb = [keep.tile([P, T], F32, name="r%d" % t) for t in range(PACK)]
 
+        gs = keep.tile([P, J], U8, name="gs", align_bytes=64)
         nc.vector.memset(ts[:].bitcast(I32), 0)
+        nc.vector.memset(gs[:].bitcast(I32), 0)
         nc.vector.memset(s4_raw[:].bitcast(I32), 0)
 
         st_rows = st.rearrange("(p t) j -> p t j", t=PACK)
         r_rows = rT.rearrange("(p t) c -> p t c", t=PACK)
         y_rows = out_0.rearrange("(p t) j -> p t j", t=PACK)
 
-        nc.sync.dma_start(offsets[:], offs)
         nc.sync.dma_start(out=wk_raw[:], in_=wk.rearrange("(p i) n -> p i n", i=PACK))
-        load_scale_rows(nc.sync, ts, tab_scales)
+        nc.sync.dma_start(offsets[:], offs)
+        nc.sync.dma_start(out=ts[0:P:8, :].bitcast(I32), in_=tab_scales[0].bitcast(I32))
         nc.sync.dma_start(out=w4_raw[:].bitcast(I32), in_=wv4_words[0].bitcast(I32))
-        nc.sync.dma_start(out=tw[:].bitcast(I32), in_=tab_words[0].rearrange("p t i -> p (t i)").bitcast(I32))
-        load_scale_rows(nc.sync, s4_raw, wv4_scales)
-        nc.sync.dma_start(out=st_sb[0][:], in_=st_rows[:, 0, :])
         nc.sync.dma_start(out=wd_raw[:], in_=wvd.rearrange("(p i) n -> p i n", i=PACK))
-        for t in range(1, PACK):
+        load_scale_rows(nc.sync, s4_raw, wv4_scales)
+        nc.sync.dma_start(out=tw[:].bitcast(I32), in_=tab_words[0].rearrange("p t i -> p (t i)").bitcast(I32))
+
+        picked = keep.tile([P, J], U8, name="picked", align_bytes=64)
+        nc.vector.tensor_copy(picked[:], ts[:].indirect(offsets[:]))
+        for q in range(4):
+            nc.sync.dma_start(out=gs[32 * q : 32 * q + 4, :].bitcast(I32), in_=picked[32 * q : 32 * q + 32 : 8, :].bitcast(I32))
+
+        for t in range(PACK):
             nc.sync.dma_start(out=st_sb[t][:], in_=st_rows[:, t, :])
         for t in range(PACK):
             nc.sync.dma_start(out=r_sb[t][:], in_=r_rows[:, t, :])
@@ -85,8 +92,6 @@ def tile_list_engram_dl_sigLP_kernel(
 
         wk_grouped = round_weight(wk_raw, "wk_grouped")
 
-        gs = keep.tile([P, J], U8, name="gs", align_bytes=64)
-        nc.vector.tensor_copy(gs[:], ts[:].indirect(offsets[:]))
 
         w4 = keep.tile([P, 2 * N], U8, name="w4", align_bytes=64)
         s4 = keep.tile([P, N], U8, name="s4", align_bytes=64)
@@ -96,16 +101,16 @@ def tile_list_engram_dl_sigLP_kernel(
         )
         wk_codes, wk_scales = quantise_weight(wk_grouped, "wk")
 
-        gw = [keep.tile([P, HALF], U32, name="gw%d" % h, align_bytes=64) for h in range(2)]
-        for h in range(2):
-            nc.vector.tensor_copy(gw[h][:], tw[:].indirect(offsets[:, h * HALF // 16 : (h + 1) * HALF // 16]))
-
         nc.vector.tensor_copy(
             out=s4[:].rearrange("p (t m) -> p m t", t=PACK),
             in_=s4_raw[:].rearrange("p (m t) -> p m t", t=PACK),
         )
         wd_grouped = round_weight(wd_raw, "wd_grouped")
         wd_codes, wd_scales = quantise_weight(wd_grouped, "wd")
+
+        gw = [keep.tile([P, HALF], U32, name="gw%d" % h, align_bytes=64) for h in range(2)]
+        for h in range(2):
+            nc.vector.tensor_copy(gw[h][:], tw[:].indirect(offsets[:, h * HALF // 16 : (h + 1) * HALF // 16]))
 
         gv = [keep.tile([P, J], F32, name="gv%d" % t) for t in range(PACK)]
         units = [(t, h) for t in range(PACK) for h in range(2)]
@@ -120,7 +125,12 @@ def tile_list_engram_dl_sigLP_kernel(
                 rhs=gw[h][:].bitcast(FP8X4), rhs_scale=gs[:, cols], start=True, stop=True,
             )
             z = ring.tile([P, HALF], F32, name="z")
-            nc.vector.tensor_tensor(z[:], ke[:], st_sb[t][:, cols], MULT)
+            if h == 0:
+                ke_sb = keep.tile([P, HALF], F32, name="ke_sb%d" % t)
+                nc.scalar.copy(out=ke_sb[:], in_=ke[:])
+                nc.gpsimd.tensor_tensor(z[:], ke_sb[:], st_sb[t][:, cols], MULT)
+            else:
+                nc.vector.tensor_tensor(z[:], ke[:], st_sb[t][:, cols], MULT)
             gate = ring.tile([P, HALF], F32, name="gate")
             nc.scalar.activation(gate[:], z[:], SIGMOID)
             gates[(t, h)] = gate
@@ -139,30 +149,26 @@ def tile_list_engram_dl_sigLP_kernel(
             )
             nc.vector.tensor_tensor(gv[t][:, cols], ve[:], gates[(t, h)][:], MULT)
 
-        make_gate(*units[0])
-        make_gate(*units[1])
-        for u in range(len(units)):
-            if u + 2 < len(units):
-                make_gate(*units[u + 2])
-            make_value(*units[u])
+        for t, h in units:
+            make_gate(t, h)
+        for t, h in units:
+            make_value(t, h)
 
-        y01 = keep.tile([P, 2, J], F32, name="y01")
-        for t in range(2):
-            nc.vector.tensor_tensor(y01[:, t, :], r_sb[t][:].indirect(offsets[:]), gv[t][:], ADD)
-        nc.sync.dma_start(out=y_rows[:, 0:2, :], in_=y01[:])
-
+        y = [keep.tile([P, 2 * J], F32, name="y%d" % u) for u in range(2)]
         yb = [keep.tile([P, b - a, PACK], BF16, name="yb%d" % a, align_bytes=64) for a, b in CHUNKS]
-        y23 = [keep.tile([P, 2, b - a], F32, name="y23_%d" % a) for a, b in CHUNKS]
-        for c, (a, b) in enumerate(CHUNKS):
-            nc.scalar.copy(out=yb[c][:, :, 0:2], in_=y01[:, :, a:b].rearrange("p t j -> p j t"))
-        for t in range(2, PACK):
-            for c, (a, b) in enumerate(CHUNKS):
+        for t in range(PACK):
+            last = t == PACK - 1
+            u, base = t // 2, (t % 2) * J
+            for a, b in CHUNKS if last else [(0, J)]:
                 nc.vector.tensor_tensor(
-                    y23[c][:, t - 2, :], r_sb[t][:].indirect(offsets[:, a // 16 : b // 16]), gv[t][:, a:b], ADD
+                    y[u][:, base + a : base + b], r_sb[t][:].indirect(offsets[:, a // 16 : b // 16]), gv[t][:, a:b], ADD
                 )
-        for c, (a, b) in enumerate(CHUNKS):
-            nc.scalar.copy(out=yb[c][:, :, 2:4], in_=y23[c][:].rearrange("p t j -> p j t"))
-            nc.sync.dma_start(out=y_rows[:, 2:4, a:b], in_=y23[c][:])
+            if t % 2 == 1:
+                pair = y[u][:].rearrange("p (e j) -> p j e", e=2)
+                for c, (a, b) in enumerate(CHUNKS):
+                    nc.scalar.copy(out=yb[c][:, :, 2 * u : 2 * u + 2], in_=pair[:, a:b, :])
+            for a, b in [(0, 640), (640, J)] if last else [(0, J)]:
+                nc.sync.dma_start(out=y_rows[:, t, a:b], in_=y[u][:, base + a : base + b])
 
         y_codes = keep.tile([P, J], U32, name="y_codes", align_bytes=64)
         y_scales = keep.tile([P, J], U8, name="y_scales", align_bytes=64)
@@ -171,9 +177,8 @@ def tile_list_engram_dl_sigLP_kernel(
             nc.vector.quantize_mx(
                 out=y_codes[:, a:b].bitcast(FP8X4), scales=y_scales[:, a:b], in_=yb[c][:].rearrange("p j t -> p (j t)")
             )
+        for a, b in [(0, 640), (640, J)]:
             nc.sync.dma_start(out=word_rows[:, a:b], in_=y_codes[:, a:b].bitcast(I32))
-        for q in range(4):
-            queue = nc.sync if q % 2 == 0 else nc.scalar
-            queue.dma_start(
-                out=out_2[0, 4 * q : 4 * q + 4, :].bitcast(I32), in_=y_scales[32 * q : 32 * q + 4, :].bitcast(I32)
-            )
+        for r in range(4):
+            queue = nc.sync if r % 2 == 0 else nc.scalar
+            queue.dma_start(out=out_2[0, r:16:4, :].bitcast(I32), in_=y_scales[r:P:32, :].bitcast(I32))

@@ -20,7 +20,8 @@ SIGMOID = mybir.ActivationFunctionType.Sigmoid
 P = 128
 PACK = 4
 HALF = 512
-CHUNKS = [(0, 128), (128, 384), (384, 640), (640, 896), (896, 1024)]
+CHUNKS = [(0, 128), (128, 384), (384, 512), (512, 768), (768, 1024)]
+VECTOR_CHUNK = 2
 
 
 def load_scale_rows(queue, plane, rows):
@@ -44,7 +45,8 @@ def tile_list_engram_dl_sigLP_kernel(
         wd_raw = keep.tile([P, PACK, N], F32, name="wd_raw")
         w4_raw = keep.tile([P, 2 * N], U8, name="w4_raw", align_bytes=64)
         s4_raw = keep.tile([P, N], U8, name="s4_raw", align_bytes=64)
-        st_sb = [keep.tile([P, J], F32, name="st%d" % t) for t in range(PACK)]
+        st_pair = [keep.tile([P, 2 * J], F32, name="st%d" % u) for u in range(2)]
+        st_sb = [st_pair[t // 2][:, (t % 2) * J : (t % 2 + 1) * J] for t in range(PACK)]
         r_sb = [keep.tile([P, T], F32, name="r%d" % t) for t in range(PACK)]
 
         gs = keep.tile([P, J], U8, name="gs", align_bytes=64)
@@ -52,13 +54,11 @@ def tile_list_engram_dl_sigLP_kernel(
         nc.vector.memset(gs[:].bitcast(I32), 0)
         nc.vector.memset(s4_raw[:].bitcast(I32), 0)
 
-        st_rows = st.rearrange("(p t) j -> p t j", t=PACK)
         r_rows = rT.rearrange("(p t) c -> p t c", t=PACK)
-        y_rows = out_0.rearrange("(p t) j -> p t j", t=PACK)
 
         nc.sync.dma_start(out=wk_raw[:], in_=wk.rearrange("(p i) n -> p i n", i=PACK))
         nc.sync.dma_start(offsets[:], offs)
-        nc.sync.dma_start(out=ts[0:P:8, :].bitcast(I32), in_=tab_scales[0].bitcast(I32))
+        nc.sync.dma_start(out=ts[4:P:8, :].bitcast(I32), in_=tab_scales[0].bitcast(I32))
         nc.sync.dma_start(out=w4_raw[:].bitcast(I32), in_=wv4_words[0].bitcast(I32))
         nc.sync.dma_start(out=wd_raw[:], in_=wvd.rearrange("(p i) n -> p i n", i=PACK))
         load_scale_rows(nc.sync, s4_raw, wv4_scales)
@@ -66,11 +66,12 @@ def tile_list_engram_dl_sigLP_kernel(
 
         picked = keep.tile([P, J], U8, name="picked", align_bytes=64)
         nc.vector.tensor_copy(picked[:], ts[:].indirect(offsets[:]))
-        for q in range(4):
-            nc.sync.dma_start(out=gs[32 * q : 32 * q + 4, :].bitcast(I32), in_=picked[32 * q : 32 * q + 32 : 8, :].bitcast(I32))
+        for r in range(4):
+            nc.sync.dma_start(out=gs[r:P:32, :].bitcast(I32), in_=picked[8 * r + 4 : P : 32, :].bitcast(I32))
 
-        for t in range(PACK):
-            nc.sync.dma_start(out=st_sb[t][:], in_=st_rows[:, t, :])
+        st_rows = st.rearrange("(p t) j -> p (t j)", t=PACK)
+        for u in range(2):
+            nc.sync.dma_start(out=st_pair[u][:], in_=st_rows[:, 2 * u * J : 2 * (u + 1) * J])
         for t in range(PACK):
             nc.sync.dma_start(out=r_sb[t][:], in_=r_rows[:, t, :])
 
@@ -113,7 +114,6 @@ def tile_list_engram_dl_sigLP_kernel(
             nc.vector.tensor_copy(gw[h][:], tw[:].indirect(offsets[:, h * HALF // 16 : (h + 1) * HALF // 16]))
 
         gv = [keep.tile([P, J], F32, name="gv%d" % t) for t in range(PACK)]
-        units = [(t, h) for t in range(PACK) for h in range(2)]
         gates = {}
 
         def make_gate(t, h):
@@ -125,12 +125,7 @@ def tile_list_engram_dl_sigLP_kernel(
                 rhs=gw[h][:].bitcast(FP8X4), rhs_scale=gs[:, cols], start=True, stop=True,
             )
             z = ring.tile([P, HALF], F32, name="z")
-            if h == 0:
-                ke_sb = keep.tile([P, HALF], F32, name="ke_sb%d" % t)
-                nc.scalar.copy(out=ke_sb[:], in_=ke[:])
-                nc.gpsimd.tensor_tensor(z[:], ke_sb[:], st_sb[t][:, cols], MULT)
-            else:
-                nc.vector.tensor_tensor(z[:], ke[:], st_sb[t][:, cols], MULT)
+            nc.vector.tensor_tensor(z[:], ke[:], st_sb[t][:, cols], MULT)
             gate = ring.tile([P, HALF], F32, name="gate")
             nc.scalar.activation(gate[:], z[:], SIGMOID)
             gates[(t, h)] = gate
@@ -149,36 +144,56 @@ def tile_list_engram_dl_sigLP_kernel(
             )
             nc.vector.tensor_tensor(gv[t][:, cols], ve[:], gates[(t, h)][:], MULT)
 
-        for t, h in units:
-            make_gate(t, h)
-        for t, h in units:
-            make_value(t, h)
+        for t in range(PACK + 1):
+            for h in range(2):
+                if t < PACK:
+                    make_gate(t, h)
+            for h in range(2):
+                if t > 0:
+                    make_value(t - 1, h)
 
-        y = [keep.tile([P, 2 * J], F32, name="y%d" % u) for u in range(2)]
+        y = keep.tile([P, PACK * J], F32, name="y")
         yb = [keep.tile([P, b - a, PACK], BF16, name="yb%d" % a, align_bytes=64) for a, b in CHUNKS]
-        for t in range(PACK):
-            last = t == PACK - 1
-            u, base = t // 2, (t % 2) * J
-            for a, b in CHUNKS if last else [(0, J)]:
-                nc.vector.tensor_tensor(
-                    y[u][:, base + a : base + b], r_sb[t][:].indirect(offsets[:, a // 16 : b // 16]), gv[t][:, a:b], ADD
-                )
-            if t % 2 == 1:
-                pair = y[u][:].rearrange("p (e j) -> p j e", e=2)
-                for c, (a, b) in enumerate(CHUNKS):
-                    nc.scalar.copy(out=yb[c][:, :, 2 * u : 2 * u + 2], in_=pair[:, a:b, :])
-            for a, b in [(0, 640), (640, J)] if last else [(0, J)]:
-                nc.sync.dma_start(out=y_rows[:, t, a:b], in_=y[u][:, base + a : base + b])
-
         y_codes = keep.tile([P, J], U32, name="y_codes", align_bytes=64)
         y_scales = keep.tile([P, J], U8, name="y_scales", align_bytes=64)
+        y_rows = out_0.rearrange("(p t) j -> p (t j)", t=PACK)
         word_rows = out_1[0].rearrange("p j i -> p (j i)").bitcast(I32)
-        for c, (a, b) in enumerate(CHUNKS):
-            nc.vector.quantize_mx(
-                out=y_codes[:, a:b].bitcast(FP8X4), scales=y_scales[:, a:b], in_=yb[c][:].rearrange("p j t -> p (j t)")
+
+        def add_record(t, a, b):
+            nc.vector.tensor_tensor(
+                y[:, t * J + a : t * J + b], r_sb[t][:].indirect(offsets[:, a // 16 : b // 16]), gv[t][:, a:b], ADD
             )
-        for a, b in [(0, 640), (640, J)]:
-            nc.sync.dma_start(out=word_rows[:, a:b], in_=y_codes[:, a:b].bitcast(I32))
+
+        def round_pair(u, c, copy):
+            a, b = CHUNKS[c]
+            pair = y[:, 2 * u * J : 2 * (u + 1) * J].rearrange("p (e j) -> p j e", e=2)
+            copy(out=yb[c][:, :, 2 * u : 2 * u + 2], in_=pair[:, a:b, :])
+
+        def quantise_chunk(c):
+            a, b = CHUNKS[c]
+            nc.vector.quantize_mx(
+                out=y_codes[:, a:b].bitcast(FP8X4), scales=y_scales[8:P, a:b], in_=yb[c][:].rearrange("p j t -> p (j t)")
+            )
+
+        add_record(0, 0, J)
+        add_record(1, 0, J)
+        for c in range(len(CHUNKS)):
+            round_pair(0, c, nc.scalar.copy)
+        add_record(2, 0, J)
+        nc.sync.dma_start(out=y_rows[:, 0 : 3 * J], in_=y[:, 0 : 3 * J])
+        for c, (a, b) in enumerate(CHUNKS):
+            add_record(3, a, b)
+            if c != VECTOR_CHUNK:
+                round_pair(1, c, nc.scalar.copy)
+            if b % HALF == 0:
+                nc.sync.dma_start(out=y_rows[:, 3 * J + b - HALF : 3 * J + b], in_=y[:, 3 * J + b - HALF : 3 * J + b])
+        quantise_chunk(0)
+        round_pair(1, VECTOR_CHUNK, nc.vector.tensor_copy)
+        for c in range(1, len(CHUNKS)):
+            quantise_chunk(c)
+            b = CHUNKS[c][1]
+            if b % HALF == 0:
+                nc.sync.dma_start(out=word_rows[:, b - HALF : b], in_=y_codes[:, b - HALF : b].bitcast(I32))
         for r in range(4):
             queue = nc.sync if r % 2 == 0 else nc.scalar
-            queue.dma_start(out=out_2[0, r:16:4, :].bitcast(I32), in_=y_scales[r:P:32, :].bitcast(I32))
+            queue.dma_start(out=out_2[0, r:16:4, :].bitcast(I32), in_=y_scales[8 + r : P : 32, :].bitcast(I32))

@@ -116,7 +116,7 @@ def tile_list_engram_dl_sigLP_kernel(
         gv = [keep.tile([P, J], F32, name="gv%d" % t) for t in range(PACK)]
         gates = {}
 
-        def make_gate(t, h):
+        def make_key(t, h):
             cols = slice(h * HALF, (h + 1) * HALF)
             ms = slice(t * P, (t + 1) * P)
             ke = psum.tile([P, HALF], F32, name="ke")
@@ -124,8 +124,11 @@ def tile_list_engram_dl_sigLP_kernel(
                 out=ke[:], lhsT=wk_codes[:, ms].bitcast(FP8X4), lhsT_scale=wk_scales[:, ms],
                 rhs=gw[h][:].bitcast(FP8X4), rhs_scale=gs[:, cols], start=True, stop=True,
             )
+            return ke
+
+        def make_gate(t, h, ke, engine):
             z = ring.tile([P, HALF], F32, name="z")
-            nc.vector.tensor_tensor(z[:], ke[:], st_sb[t][:, cols], MULT)
+            engine.tensor_tensor(z[:], ke[:], st_sb[t][:, h * HALF : (h + 1) * HALF], MULT)
             gate = ring.tile([P, HALF], F32, name="gate")
             nc.scalar.activation(gate[:], z[:], SIGMOID)
             gates[(t, h)] = gate
@@ -144,13 +147,15 @@ def tile_list_engram_dl_sigLP_kernel(
             )
             nc.vector.tensor_tensor(gv[t][:, cols], ve[:], gates[(t, h)][:], MULT)
 
-        for t in range(PACK + 1):
-            for h in range(2):
-                if t < PACK:
-                    make_gate(t, h)
-            for h in range(2):
-                if t > 0:
-                    make_value(t - 1, h)
+        ke_sb = [keep.tile([P, HALF], F32, name="ke_sb%d" % t) for t in range(PACK)]
+        for t in range(PACK):
+            nc.scalar.copy(out=ke_sb[t][:], in_=make_key(t, 0)[:])
+        for t in range(PACK):
+            make_gate(t, 1, make_key(t, 1), nc.vector)
+            make_gate(t, 0, ke_sb[t], nc.gpsimd)
+        for h in (1, 0):
+            for t in range(PACK):
+                make_value(t, h)
 
         y = keep.tile([P, PACK * J], F32, name="y")
         yb = [keep.tile([P, b - a, PACK], BF16, name="yb%d" % a, align_bytes=64) for a, b in CHUNKS]
@@ -175,25 +180,30 @@ def tile_list_engram_dl_sigLP_kernel(
                 out=y_codes[:, a:b].bitcast(FP8X4), scales=y_scales[8:P, a:b], in_=yb[c][:].rearrange("p j t -> p (j t)")
             )
 
+        def store_y(a, b):
+            nc.sync.dma_start(out=y_rows[:, a:b], in_=y[:, a:b])
+
         add_record(0, 0, J)
         add_record(1, 0, J)
+        store_y(0, 2 * J)
         for c in range(len(CHUNKS)):
             round_pair(0, c, nc.scalar.copy)
         add_record(2, 0, J)
-        nc.sync.dma_start(out=y_rows[:, 0 : 3 * J], in_=y[:, 0 : 3 * J])
         for c, (a, b) in enumerate(CHUNKS):
             add_record(3, a, b)
             if c != VECTOR_CHUNK:
                 round_pair(1, c, nc.scalar.copy)
-            if b % HALF == 0:
-                nc.sync.dma_start(out=y_rows[:, 3 * J + b - HALF : 3 * J + b], in_=y[:, 3 * J + b - HALF : 3 * J + b])
+            if c == 0:
+                store_y(2 * J, 3 * J + b)
+        store_y(3 * J + CHUNKS[0][1], 4 * J)
         quantise_chunk(0)
         round_pair(1, VECTOR_CHUNK, nc.vector.tensor_copy)
         for c in range(1, len(CHUNKS)):
             quantise_chunk(c)
-            b = CHUNKS[c][1]
-            if b % HALF == 0:
-                nc.sync.dma_start(out=word_rows[:, b - HALF : b], in_=y_codes[:, b - HALF : b].bitcast(I32))
+            if c >= VECTOR_CHUNK:
+                a = 0 if c == VECTOR_CHUNK else CHUNKS[c][0]
+                b = CHUNKS[c][1]
+                nc.sync.dma_start(out=word_rows[:, a:b], in_=y_codes[:, a:b].bitcast(I32))
         for r in range(4):
             queue = nc.sync if r % 2 == 0 else nc.scalar
             queue.dma_start(out=out_2[0, r:16:4, :].bitcast(I32), in_=y_scales[8 + r : P : 32, :].bitcast(I32))

@@ -20,8 +20,7 @@ SIGMOID = mybir.ActivationFunctionType.Sigmoid
 P = 128
 PACK = 4
 HALF = 512
-CHUNKS = [(0, 128), (128, 384), (384, 512), (512, 768), (768, 1024)]
-VECTOR_CHUNK = 2
+CHUNKS = [(0, 128), (128, 384), (384, 640), (640, 896), (896, 1024)]
 
 
 def load_scale_rows(queue, plane, rows):
@@ -45,8 +44,8 @@ def tile_list_engram_dl_sigLP_kernel(
         wd_raw = keep.tile([P, PACK, N], F32, name="wd_raw")
         w4_raw = keep.tile([P, 2 * N], U8, name="w4_raw", align_bytes=64)
         s4_raw = keep.tile([P, N], U8, name="s4_raw", align_bytes=64)
-        st_pair = [keep.tile([P, 2 * J], F32, name="st%d" % u) for u in range(2)]
-        st_sb = [st_pair[t // 2][:, (t % 2) * J : (t % 2 + 1) * J] for t in range(PACK)]
+        st_all = keep.tile([P, PACK * J], F32, name="st_all")
+        st_sb = [st_all[:, t * J : (t + 1) * J] for t in range(PACK)]
         r_sb = [keep.tile([P, T], F32, name="r%d" % t) for t in range(PACK)]
 
         gs = keep.tile([P, J], U8, name="gs", align_bytes=64)
@@ -69,9 +68,7 @@ def tile_list_engram_dl_sigLP_kernel(
         for r in range(4):
             nc.sync.dma_start(out=gs[r:P:32, :].bitcast(I32), in_=picked[8 * r + 4 : P : 32, :].bitcast(I32))
 
-        st_rows = st.rearrange("(p t) j -> p (t j)", t=PACK)
-        for u in range(2):
-            nc.sync.dma_start(out=st_pair[u][:], in_=st_rows[:, 2 * u * J : 2 * (u + 1) * J])
+        nc.sync.dma_start(out=st_all[:], in_=st.rearrange("(p t) j -> p (t j)", t=PACK))
         for t in range(PACK):
             nc.sync.dma_start(out=r_sb[t][:], in_=r_rows[:, t, :])
 
@@ -191,19 +188,14 @@ def tile_list_engram_dl_sigLP_kernel(
         add_record(2, 0, J)
         for c, (a, b) in enumerate(CHUNKS):
             add_record(3, a, b)
-            if c != VECTOR_CHUNK:
-                round_pair(1, c, nc.scalar.copy)
+            round_pair(1, c, nc.scalar.copy)
             if c == 0:
                 store_y(2 * J, 3 * J + b)
         store_y(3 * J + CHUNKS[0][1], 4 * J)
-        quantise_chunk(0)
-        round_pair(1, VECTOR_CHUNK, nc.vector.tensor_copy)
-        for c in range(1, len(CHUNKS)):
+        for c in range(len(CHUNKS)):
             quantise_chunk(c)
-            if c >= VECTOR_CHUNK:
-                a = 0 if c == VECTOR_CHUNK else CHUNKS[c][0]
-                b = CHUNKS[c][1]
-                nc.sync.dma_start(out=word_rows[:, a:b], in_=y_codes[:, a:b].bitcast(I32))
+        for a, b in [(0, 640), (640, 896), (896, J)]:
+            nc.sync.dma_start(out=word_rows[:, a:b], in_=y_codes[:, a:b].bitcast(I32))
         for r in range(4):
             queue = nc.sync if r % 2 == 0 else nc.scalar
             queue.dma_start(out=out_2[0, r:16:4, :].bitcast(I32), in_=y_scales[8 + r : P : 32, :].bitcast(I32))

@@ -44,31 +44,33 @@ def tile_list_engram_dl_sigLP_kernel(
         wd_raw = keep.tile([P, PACK, N], F32, name="wd_raw")
         w4_raw = keep.tile([P, 2 * N], U8, name="w4_raw", align_bytes=64)
         s4_raw = keep.tile([P, N], U8, name="s4_raw", align_bytes=64)
-        st_all = keep.tile([P, PACK * J], F32, name="st_all")
-        st_sb = [st_all[:, t * J : (t + 1) * J] for t in range(PACK)]
+        st_pair = [keep.tile([P, 2 * J], F32, name="st%d" % u) for u in range(2)]
+        st_sb = [st_pair[t // 2][:, (t % 2) * J : (t % 2 + 1) * J] for t in range(PACK)]
         r_sb = [keep.tile([P, T], F32, name="r%d" % t) for t in range(PACK)]
 
         gs = keep.tile([P, J], U8, name="gs", align_bytes=64)
+        nc.vector.memset(s4_raw[:].bitcast(I32), 0)
         nc.vector.memset(ts[:].bitcast(I32), 0)
         nc.vector.memset(gs[:].bitcast(I32), 0)
-        nc.vector.memset(s4_raw[:].bitcast(I32), 0)
 
         r_rows = rT.rearrange("(p t) c -> p t c", t=PACK)
+        st_rows = st.rearrange("(p t) j -> p (t j)", t=PACK)
 
         nc.sync.dma_start(out=wk_raw[:], in_=wk.rearrange("(p i) n -> p i n", i=PACK))
         nc.sync.dma_start(offsets[:], offs)
-        nc.sync.dma_start(out=ts[4:P:8, :].bitcast(I32), in_=tab_scales[0].bitcast(I32))
-        nc.sync.dma_start(out=w4_raw[:].bitcast(I32), in_=wv4_words[0].bitcast(I32))
-        nc.sync.dma_start(out=wd_raw[:], in_=wvd.rearrange("(p i) n -> p i n", i=PACK))
         load_scale_rows(nc.sync, s4_raw, wv4_scales)
+        nc.sync.dma_start(out=ts[4:P:8, :].bitcast(I32), in_=tab_scales[0].bitcast(I32))
         nc.sync.dma_start(out=tw[:].bitcast(I32), in_=tab_words[0].rearrange("p t i -> p (t i)").bitcast(I32))
+        nc.sync.dma_start(out=wd_raw[:], in_=wvd.rearrange("(p i) n -> p i n", i=PACK))
+        nc.sync.dma_start(out=w4_raw[:].bitcast(I32), in_=wv4_words[0].bitcast(I32))
+        nc.sync.dma_start(out=st_pair[0][:], in_=st_rows[:, 0 : 2 * J])
 
         picked = keep.tile([P, J], U8, name="picked", align_bytes=64)
         nc.vector.tensor_copy(picked[:], ts[:].indirect(offsets[:]))
         for r in range(4):
             nc.sync.dma_start(out=gs[r:P:32, :].bitcast(I32), in_=picked[8 * r + 4 : P : 32, :].bitcast(I32))
 
-        nc.sync.dma_start(out=st_all[:], in_=st.rearrange("(p t) j -> p (t j)", t=PACK))
+        nc.sync.dma_start(out=st_pair[1][:], in_=st_rows[:, 2 * J : 4 * J])
         for t in range(PACK):
             nc.sync.dma_start(out=r_sb[t][:], in_=r_rows[:, t, :])
 
@@ -89,26 +91,23 @@ def tile_list_engram_dl_sigLP_kernel(
             return codes, scales
 
         wk_grouped = round_weight(wk_raw, "wk_grouped")
-
-
         w4 = keep.tile([P, 2 * N], U8, name="w4", align_bytes=64)
         s4 = keep.tile([P, N], U8, name="s4", align_bytes=64)
-        nc.vector.tensor_copy(
-            out=w4[:].rearrange("p (t m b) -> p m t b", t=PACK, b=2),
-            in_=w4_raw[:].rearrange("p (m t b) -> p m t b", t=PACK, b=2),
-        )
-        wk_codes, wk_scales = quantise_weight(wk_grouped, "wk")
-
         nc.vector.tensor_copy(
             out=s4[:].rearrange("p (t m) -> p m t", t=PACK),
             in_=s4_raw[:].rearrange("p (m t) -> p m t", t=PACK),
         )
-        wd_grouped = round_weight(wd_raw, "wd_grouped")
-        wd_codes, wd_scales = quantise_weight(wd_grouped, "wd")
-
+        wk_codes, wk_scales = quantise_weight(wk_grouped, "wk")
         gw = [keep.tile([P, HALF], U32, name="gw%d" % h, align_bytes=64) for h in range(2)]
         for h in range(2):
             nc.vector.tensor_copy(gw[h][:], tw[:].indirect(offsets[:, h * HALF // 16 : (h + 1) * HALF // 16]))
+
+        nc.vector.tensor_copy(
+            out=w4[:].rearrange("p (t m b) -> p m t b", t=PACK, b=2),
+            in_=w4_raw[:].rearrange("p (m t b) -> p m t b", t=PACK, b=2),
+        )
+        wd_grouped = round_weight(wd_raw, "wd_grouped")
+        wd_codes, wd_scales = quantise_weight(wd_grouped, "wd")
 
         gv = [keep.tile([P, J], F32, name="gv%d" % t) for t in range(PACK)]
         gates = {}

@@ -20,7 +20,7 @@ SIGMOID = mybir.ActivationFunctionType.Sigmoid
 P = 128
 PACK = 4
 HALF = 512
-CHUNKS = [(0, 128), (128, 384), (384, 640), (640, 896), (896, 1024)]
+CHUNKS = [(0, 128), (128, 384), (384, 640), (640, 768), (768, 1024)]
 
 
 def load_scale_rows(queue, plane, rows):
@@ -187,13 +187,19 @@ def tile_list_engram_dl_sigLP_kernel(
         add_record(2, 0, J)
         for c, (a, b) in enumerate(CHUNKS):
             add_record(3, a, b)
-            round_pair(1, c, nc.scalar.copy)
+            if c < 4:
+                round_pair(1, c, nc.scalar.copy)
             if c == 0:
                 store_y(2 * J, 3 * J + b)
-        store_y(3 * J + CHUNKS[0][1], 4 * J)
-        for c in range(len(CHUNKS)):
+            if c == 2:
+                store_y(3 * J + CHUNKS[0][1], 3 * J + b)
+        store_y(3 * J + CHUNKS[2][1], 4 * J)
+        quantise_chunk(0)
+        quantise_chunk(1)
+        round_pair(1, 4, nc.vector.tensor_copy)
+        for c in (2, 4, 3):
             quantise_chunk(c)
-        for a, b in [(0, 640), (640, 896), (896, J)]:
+        for a, b in [(0, 384), (384, 640), (640, J)]:
             nc.sync.dma_start(out=word_rows[:, a:b], in_=y_codes[:, a:b].bitcast(I32))
         for r in range(4):
             queue = nc.sync if r % 2 == 0 else nc.scalar

@@ -20,12 +20,12 @@ SIGMOID = mybir.ActivationFunctionType.Sigmoid
 P = 128
 PACK = 4
 HALF = 512
+
 CHUNKS = [(0, 128), (128, 384), (384, 640), (640, 768), (768, 1024)]
+SCALAR_LAST, VECTOR_CHUNK = 3, 4
 
-
-def load_scale_rows(queue, plane, rows):
-    for r in range(4):
-        queue.dma_start(out=plane[r:P:32, :].bitcast(I32), in_=rows[0, r:16:4, :].bitcast(I32))
+STAGE_ROW = 4
+OUT_PLANE = 8
 
 
 def tile_list_engram_dl_sigLP_kernel(
@@ -58,8 +58,9 @@ def tile_list_engram_dl_sigLP_kernel(
 
         nc.sync.dma_start(out=wk_raw[:], in_=wk.rearrange("(p i) n -> p i n", i=PACK))
         nc.sync.dma_start(offsets[:], offs)
-        load_scale_rows(nc.sync, s4_raw, wv4_scales)
-        nc.sync.dma_start(out=ts[4:P:8, :].bitcast(I32), in_=tab_scales[0].bitcast(I32))
+        for r in range(4):
+            nc.sync.dma_start(out=s4_raw[r:P:32, :].bitcast(I32), in_=wv4_scales[0, r:16:4, :].bitcast(I32))
+        nc.sync.dma_start(out=ts[STAGE_ROW:P:8, :].bitcast(I32), in_=tab_scales[0].bitcast(I32))
         nc.sync.dma_start(out=tw[:].bitcast(I32), in_=tab_words[0].rearrange("p t i -> p (t i)").bitcast(I32))
         nc.sync.dma_start(out=wd_raw[:], in_=wvd.rearrange("(p i) n -> p i n", i=PACK))
         nc.sync.dma_start(out=w4_raw[:].bitcast(I32), in_=wv4_words[0].bitcast(I32))
@@ -68,7 +69,9 @@ def tile_list_engram_dl_sigLP_kernel(
         picked = keep.tile([P, J], U8, name="picked", align_bytes=64)
         nc.vector.tensor_copy(picked[:], ts[:].indirect(offsets[:]))
         for r in range(4):
-            nc.sync.dma_start(out=gs[r:P:32, :].bitcast(I32), in_=picked[8 * r + 4 : P : 32, :].bitcast(I32))
+            nc.sync.dma_start(
+                out=gs[r:P:32, :].bitcast(I32), in_=picked[8 * r + STAGE_ROW : P : 32, :].bitcast(I32)
+            )
 
         nc.sync.dma_start(out=st_pair[1][:], in_=st_rows[:, 2 * J : 4 * J])
         for t in range(PACK):
@@ -165,15 +168,21 @@ def tile_list_engram_dl_sigLP_kernel(
                 y[:, t * J + a : t * J + b], r_sb[t][:].indirect(offsets[:, a // 16 : b // 16]), gv[t][:, a:b], ADD
             )
 
-        def round_pair(u, c, copy):
+        def round_first_pair(c):
             a, b = CHUNKS[c]
-            pair = y[:, 2 * u * J : 2 * (u + 1) * J].rearrange("p (e j) -> p j e", e=2)
-            copy(out=yb[c][:, :, 2 * u : 2 * u + 2], in_=pair[:, a:b, :])
+            pair = y[:, 0 : 2 * J].rearrange("p (e j) -> p j e", e=2)
+            nc.scalar.copy(out=yb[c][:, :, 0:2], in_=pair[:, a:b, :])
+
+        def round_slot(t, c, copy):
+            a, b = CHUNKS[c]
+            copy(out=yb[c][:, :, t], in_=y[:, t * J + a : t * J + b])
 
         def quantise_chunk(c):
             a, b = CHUNKS[c]
             nc.vector.quantize_mx(
-                out=y_codes[:, a:b].bitcast(FP8X4), scales=y_scales[8:P, a:b], in_=yb[c][:].rearrange("p j t -> p (j t)")
+                out=y_codes[:, a:b].bitcast(FP8X4),
+                scales=y_scales[OUT_PLANE:P, a:b],
+                in_=yb[c][:].rearrange("p j t -> p (j t)"),
             )
 
         def store_y(a, b):
@@ -183,24 +192,29 @@ def tile_list_engram_dl_sigLP_kernel(
         add_record(1, 0, J)
         store_y(0, 2 * J)
         for c in range(len(CHUNKS)):
-            round_pair(0, c, nc.scalar.copy)
+            round_first_pair(c)
         add_record(2, 0, J)
+        for c in range(len(CHUNKS)):
+            round_slot(2, c, nc.vector.tensor_copy)
+
+        stored = 2 * J
         for c, (a, b) in enumerate(CHUNKS):
             add_record(3, a, b)
-            if c < 4:
-                round_pair(1, c, nc.scalar.copy)
-            if c == 0:
-                store_y(2 * J, 3 * J + b)
-            if c == 2:
-                store_y(3 * J + CHUNKS[0][1], 3 * J + b)
-        store_y(3 * J + CHUNKS[2][1], 4 * J)
+            if c != VECTOR_CHUNK:
+                round_slot(3, c, nc.scalar.copy)
+            if c % 2 == 0:
+                store_y(stored, 3 * J + b)
+                stored = 3 * J + b
+
         quantise_chunk(0)
         quantise_chunk(1)
-        round_pair(1, 4, nc.vector.tensor_copy)
-        for c in (2, 4, 3):
+        round_slot(3, VECTOR_CHUNK, nc.vector.tensor_copy)
+        for c in (2, VECTOR_CHUNK, SCALAR_LAST):
             quantise_chunk(c)
-        for a, b in [(0, 384), (384, 640), (640, J)]:
+        for a, b in [(0, CHUNKS[1][1]), CHUNKS[2], (CHUNKS[SCALAR_LAST][0], J)]:
             nc.sync.dma_start(out=word_rows[:, a:b], in_=y_codes[:, a:b].bitcast(I32))
         for r in range(4):
             queue = nc.sync if r % 2 == 0 else nc.scalar
-            queue.dma_start(out=out_2[0, r:16:4, :].bitcast(I32), in_=y_scales[8 + r : P : 32, :].bitcast(I32))
+            queue.dma_start(
+                out=out_2[0, r:16:4, :].bitcast(I32), in_=y_scales[OUT_PLANE + r : P : 32, :].bitcast(I32)
+            )

@@ -49,8 +49,8 @@ def tile_list_engram_dl_sigLP_kernel(
         r_sb = [keep.tile([P, T], F32, name="r%d" % t) for t in range(PACK)]
 
         gs = keep.tile([P, J], U8, name="gs", align_bytes=64)
-        nc.vector.memset(s4_raw[:].bitcast(I32), 0)
         nc.vector.memset(ts[:].bitcast(I32), 0)
+        nc.vector.memset(s4_raw[:].bitcast(I32), 0)
         nc.vector.memset(gs[:].bitcast(I32), 0)
 
         r_rows = rT.rearrange("(p t) c -> p t c", t=PACK)
@@ -58,13 +58,12 @@ def tile_list_engram_dl_sigLP_kernel(
 
         nc.sync.dma_start(out=wk_raw[:], in_=wk.rearrange("(p i) n -> p i n", i=PACK))
         nc.sync.dma_start(offsets[:], offs)
+        nc.sync.dma_start(out=ts[STAGE_ROW:P:8, :].bitcast(I32), in_=tab_scales[0].bitcast(I32))
+        nc.sync.dma_start(out=w4_raw[:].bitcast(I32), in_=wv4_words[0].bitcast(I32))
+        nc.sync.dma_start(out=tw[:].bitcast(I32), in_=tab_words[0].rearrange("p t i -> p (t i)").bitcast(I32))
         for r in range(4):
             nc.sync.dma_start(out=s4_raw[r:P:32, :].bitcast(I32), in_=wv4_scales[0, r:16:4, :].bitcast(I32))
-        nc.sync.dma_start(out=ts[STAGE_ROW:P:8, :].bitcast(I32), in_=tab_scales[0].bitcast(I32))
-        nc.sync.dma_start(out=tw[:].bitcast(I32), in_=tab_words[0].rearrange("p t i -> p (t i)").bitcast(I32))
         nc.sync.dma_start(out=wd_raw[:], in_=wvd.rearrange("(p i) n -> p i n", i=PACK))
-        nc.sync.dma_start(out=w4_raw[:].bitcast(I32), in_=wv4_words[0].bitcast(I32))
-        nc.sync.dma_start(out=st_pair[0][:], in_=st_rows[:, 0 : 2 * J])
 
         picked = keep.tile([P, J], U8, name="picked", align_bytes=64)
         nc.vector.tensor_copy(picked[:], ts[:].indirect(offsets[:]))
@@ -73,7 +72,8 @@ def tile_list_engram_dl_sigLP_kernel(
                 out=gs[r:P:32, :].bitcast(I32), in_=picked[8 * r + STAGE_ROW : P : 32, :].bitcast(I32)
             )
 
-        nc.sync.dma_start(out=st_pair[1][:], in_=st_rows[:, 2 * J : 4 * J])
+        for u in range(2):
+            nc.sync.dma_start(out=st_pair[u][:], in_=st_rows[:, 2 * u * J : 2 * (u + 1) * J])
         for t in range(PACK):
             nc.sync.dma_start(out=r_sb[t][:], in_=r_rows[:, t, :])
 
@@ -94,23 +94,21 @@ def tile_list_engram_dl_sigLP_kernel(
             return codes, scales
 
         wk_grouped = round_weight(wk_raw, "wk_grouped")
+        wk_codes, wk_scales = quantise_weight(wk_grouped, "wk")
         w4 = keep.tile([P, 2 * N], U8, name="w4", align_bytes=64)
         s4 = keep.tile([P, N], U8, name="s4", align_bytes=64)
-        nc.vector.tensor_copy(
-            out=s4[:].rearrange("p (t m) -> p m t", t=PACK),
-            in_=s4_raw[:].rearrange("p (m t) -> p m t", t=PACK),
-        )
-        wk_codes, wk_scales = quantise_weight(wk_grouped, "wk")
-        gw = [keep.tile([P, HALF], U32, name="gw%d" % h, align_bytes=64) for h in range(2)]
-        for h in range(2):
-            nc.vector.tensor_copy(gw[h][:], tw[:].indirect(offsets[:, h * HALF // 16 : (h + 1) * HALF // 16]))
-
         nc.vector.tensor_copy(
             out=w4[:].rearrange("p (t m b) -> p m t b", t=PACK, b=2),
             in_=w4_raw[:].rearrange("p (m t b) -> p m t b", t=PACK, b=2),
         )
-        wd_grouped = round_weight(wd_raw, "wd_grouped")
-        wd_codes, wd_scales = quantise_weight(wd_grouped, "wd")
+        gw = [keep.tile([P, HALF], U32, name="gw%d" % h, align_bytes=64) for h in range(2)]
+        for h in range(2):
+            nc.vector.tensor_copy(gw[h][:], tw[:].indirect(offsets[:, h * HALF // 16 : (h + 1) * HALF // 16]))
+        nc.vector.tensor_copy(
+            out=s4[:].rearrange("p (t m) -> p m t", t=PACK),
+            in_=s4_raw[:].rearrange("p (m t) -> p m t", t=PACK),
+        )
+        wd_codes, wd_scales = quantise_weight(round_weight(wd_raw, "wd_grouped"), "wd")
 
         gv = [keep.tile([P, J], F32, name="gv%d" % t) for t in range(PACK)]
         gates = {}
@@ -146,14 +144,20 @@ def tile_list_engram_dl_sigLP_kernel(
             )
             nc.vector.tensor_tensor(gv[t][:, cols], ve[:], gates[(t, h)][:], MULT)
 
-        ke_sb = [keep.tile([P, HALF], F32, name="ke_sb%d" % t) for t in range(PACK)]
-        for t in range(PACK):
-            nc.scalar.copy(out=ke_sb[t][:], in_=make_key(t, 0)[:])
-        for t in range(PACK):
-            make_gate(t, 1, make_key(t, 1), nc.vector)
-            make_gate(t, 0, ke_sb[t], nc.gpsimd)
-        for h in (1, 0):
-            for t in range(PACK):
+        ke_sb = [keep.tile([P, HALF], F32, name="ke_sb%d" % h) for h in range(2)]
+        for h in range(2):
+            nc.scalar.copy(out=ke_sb[h][:], in_=make_key(3, h)[:])
+        for t in range(2):
+            for h in range(2):
+                make_gate(t, h, make_key(t, h), nc.vector)
+        for t in range(2):
+            for h in range(2):
+                make_value(t, h)
+        for h in range(2):
+            make_gate(3, h, ke_sb[h], nc.gpsimd)
+            make_gate(2, h, make_key(2, h), nc.vector)
+        for t in (2, 3):
+            for h in range(2):
                 make_value(t, h)
 
         y = keep.tile([P, PACK * J], F32, name="y")
@@ -190,28 +194,30 @@ def tile_list_engram_dl_sigLP_kernel(
 
         add_record(0, 0, J)
         add_record(1, 0, J)
-        store_y(0, 2 * J)
         for c in range(len(CHUNKS)):
             round_first_pair(c)
         add_record(2, 0, J)
-        for c in range(len(CHUNKS)):
+        store_y(0, 3 * J)
+        for c in (VECTOR_CHUNK, 0, 1):
             round_slot(2, c, nc.vector.tensor_copy)
+        for c in (2, SCALAR_LAST):
+            round_slot(2, c, nc.scalar.copy)
 
-        stored = 2 * J
+        stored = 3 * J
         for c, (a, b) in enumerate(CHUNKS):
             add_record(3, a, b)
             if c != VECTOR_CHUNK:
                 round_slot(3, c, nc.scalar.copy)
-            if c % 2 == 0:
+            if c in (2, VECTOR_CHUNK):
                 store_y(stored, 3 * J + b)
                 stored = 3 * J + b
 
-        quantise_chunk(0)
-        quantise_chunk(1)
-        round_slot(3, VECTOR_CHUNK, nc.vector.tensor_copy)
-        for c in (2, VECTOR_CHUNK, SCALAR_LAST):
+        for c in (0, 1, 2):
             quantise_chunk(c)
-        for a, b in [(0, CHUNKS[1][1]), CHUNKS[2], (CHUNKS[SCALAR_LAST][0], J)]:
+        round_slot(3, VECTOR_CHUNK, nc.vector.tensor_copy)
+        for c in (SCALAR_LAST, VECTOR_CHUNK):
+            quantise_chunk(c)
+        for a, b in [(0, CHUNKS[2][1]), (CHUNKS[SCALAR_LAST][0], J)]:
             nc.sync.dma_start(out=word_rows[:, a:b], in_=y_codes[:, a:b].bitcast(I32))
         for r in range(4):
             queue = nc.sync if r % 2 == 0 else nc.scalar

@@ -24,7 +24,7 @@ HALF = 512
 CHUNKS = [(0, 128), (128, 384), (384, 640), (640, 768), (768, 1024)]
 SCALAR_LAST, VECTOR_CHUNK = 3, 4
 
-STAGE_ROW = 4
+STAGE_ROW = 32
 OUT_PLANE = 8
 
 
@@ -48,28 +48,37 @@ def tile_list_engram_dl_sigLP_kernel(
         st_sb = [st_pair[t // 2][:, (t % 2) * J : (t % 2 + 1) * J] for t in range(PACK)]
         r_sb = [keep.tile([P, T], F32, name="r%d" % t) for t in range(PACK)]
 
-        gs = keep.tile([P, J], U8, name="gs", align_bytes=64)
+        planes = keep.tile([P, J + N], U8, name="planes", align_bytes=64)
+        gs = planes[:, 0:J]
+        s4 = planes[:, J : J + N]
         nc.vector.memset(ts[:].bitcast(I32), 0)
         nc.vector.memset(s4_raw[:].bitcast(I32), 0)
-        nc.vector.memset(gs[:].bitcast(I32), 0)
+        nc.vector.memset(planes[:].bitcast(I32), 0)
 
         r_rows = rT.rearrange("(p t) c -> p t c", t=PACK)
         st_rows = st.rearrange("(p t) j -> p (t j)", t=PACK)
 
         nc.sync.dma_start(out=wk_raw[:], in_=wk.rearrange("(p i) n -> p i n", i=PACK))
         nc.sync.dma_start(offsets[:], offs)
-        nc.sync.dma_start(out=ts[STAGE_ROW:P:8, :].bitcast(I32), in_=tab_scales[0].bitcast(I32))
+        staged_rows = slice(STAGE_ROW, STAGE_ROW + 64, 4)
+        nc.sync.dma_start(out=ts[staged_rows, :].bitcast(I32), in_=tab_scales[0].bitcast(I32))
+        nc.sync.dma_start(out=s4_raw[staged_rows, :].bitcast(I32), in_=wv4_scales[0].bitcast(I32))
         nc.sync.dma_start(out=w4_raw[:].bitcast(I32), in_=wv4_words[0].bitcast(I32))
         nc.sync.dma_start(out=tw[:].bitcast(I32), in_=tab_words[0].rearrange("p t i -> p (t i)").bitcast(I32))
-        for r in range(4):
-            nc.sync.dma_start(out=s4_raw[r:P:32, :].bitcast(I32), in_=wv4_scales[0, r:16:4, :].bitcast(I32))
         nc.sync.dma_start(out=wd_raw[:], in_=wvd.rearrange("(p i) n -> p i n", i=PACK))
 
         picked = keep.tile([P, J], U8, name="picked", align_bytes=64)
         nc.vector.tensor_copy(picked[:], ts[:].indirect(offsets[:]))
+        staged = keep.tile([P, J + N], U8, name="staged", align_bytes=64)
+        nc.vector.tensor_copy(
+            out=staged[:, J : J + N].rearrange("p (t m) -> p m t", t=PACK),
+            in_=s4_raw[:].rearrange("p (m t) -> p m t", t=PACK),
+        )
+        nc.vector.tensor_copy(out=staged[:, 0:J].bitcast(I32), in_=picked[:].bitcast(I32))
         for r in range(4):
             nc.sync.dma_start(
-                out=gs[r:P:32, :].bitcast(I32), in_=picked[8 * r + STAGE_ROW : P : 32, :].bitcast(I32)
+                out=planes[r:P:32, :].bitcast(I32),
+                in_=staged[STAGE_ROW + 4 * r : STAGE_ROW + 64 : 16, :].bitcast(I32),
             )
 
         for u in range(2):
@@ -96,7 +105,6 @@ def tile_list_engram_dl_sigLP_kernel(
         wk_grouped = round_weight(wk_raw, "wk_grouped")
         wk_codes, wk_scales = quantise_weight(wk_grouped, "wk")
         w4 = keep.tile([P, 2 * N], U8, name="w4", align_bytes=64)
-        s4 = keep.tile([P, N], U8, name="s4", align_bytes=64)
         nc.vector.tensor_copy(
             out=w4[:].rearrange("p (t m b) -> p m t b", t=PACK, b=2),
             in_=w4_raw[:].rearrange("p (m t b) -> p m t b", t=PACK, b=2),
@@ -104,10 +112,6 @@ def tile_list_engram_dl_sigLP_kernel(
         gw = [keep.tile([P, HALF], U32, name="gw%d" % h, align_bytes=64) for h in range(2)]
         for h in range(2):
             nc.vector.tensor_copy(gw[h][:], tw[:].indirect(offsets[:, h * HALF // 16 : (h + 1) * HALF // 16]))
-        nc.vector.tensor_copy(
-            out=s4[:].rearrange("p (t m) -> p m t", t=PACK),
-            in_=s4_raw[:].rearrange("p (m t) -> p m t", t=PACK),
-        )
         wd_codes, wd_scales = quantise_weight(round_weight(wd_raw, "wd_grouped"), "wd")
 
         gv = [keep.tile([P, J], F32, name="gv%d" % t) for t in range(PACK)]

@@ -21,8 +21,9 @@ P = 128
 PACK = 4
 HALF = 512
 
-CHUNKS = [(0, 128), (128, 384), (384, 640), (640, 768), (768, 1024)]
-SCALAR_LAST, VECTOR_CHUNK = 3, 4
+GATHERS = [(0, 128), (128, 320), (320, 608), (608, 1024)]
+VECTOR_PIECE = (768, 896)
+SCALAR_PIECES = GATHERS[:3] + [(608, 768), (896, 1024)]
 
 STAGE_ROW = 32
 OUT_PLANE = 8
@@ -165,7 +166,8 @@ def tile_list_engram_dl_sigLP_kernel(
                 make_value(t, h)
 
         y = keep.tile([P, PACK * J], F32, name="y")
-        yb = [keep.tile([P, b - a, PACK], BF16, name="yb%d" % a, align_bytes=64) for a, b in CHUNKS]
+        yb = keep.tile([P, J * PACK], BF16, name="yb", align_bytes=64)
+        yb_slots = yb[:].rearrange("p (j t) -> p j t", t=PACK)
         y_codes = keep.tile([P, J], U32, name="y_codes", align_bytes=64)
         y_scales = keep.tile([P, J], U8, name="y_scales", align_bytes=64)
         y_rows = out_0.rearrange("(p t) j -> p (t j)", t=PACK)
@@ -176,53 +178,45 @@ def tile_list_engram_dl_sigLP_kernel(
                 y[:, t * J + a : t * J + b], r_sb[t][:].indirect(offsets[:, a // 16 : b // 16]), gv[t][:, a:b], ADD
             )
 
-        def round_first_pair(c):
-            a, b = CHUNKS[c]
-            pair = y[:, 0 : 2 * J].rearrange("p (e j) -> p j e", e=2)
-            nc.scalar.copy(out=yb[c][:, :, 0:2], in_=pair[:, a:b, :])
+        def round_slot(t, a, b, copy):
+            copy(out=yb_slots[:, a:b, t], in_=y[:, t * J + a : t * J + b])
 
-        def round_slot(t, c, copy):
-            a, b = CHUNKS[c]
-            copy(out=yb[c][:, :, t], in_=y[:, t * J + a : t * J + b])
-
-        def quantise_chunk(c):
-            a, b = CHUNKS[c]
+        def quantise(a, b):
             nc.vector.quantize_mx(
-                out=y_codes[:, a:b].bitcast(FP8X4),
-                scales=y_scales[OUT_PLANE:P, a:b],
-                in_=yb[c][:].rearrange("p j t -> p (j t)"),
+                out=y_codes[:, a:b].bitcast(FP8X4), scales=y_scales[OUT_PLANE:P, a:b], in_=yb[:, PACK * a : PACK * b]
             )
+
+        def store_words(a, b):
+            nc.sync.dma_start(out=word_rows[:, a:b], in_=y_codes[:, a:b].bitcast(I32))
 
         def store_y(a, b):
             nc.sync.dma_start(out=y_rows[:, a:b], in_=y[:, a:b])
 
         add_record(0, 0, J)
         add_record(1, 0, J)
-        for c in range(len(CHUNKS)):
-            round_first_pair(c)
+        nc.scalar.copy(out=yb_slots[:, :, 0:2], in_=y[:, 0 : 2 * J].rearrange("p (e j) -> p j e", e=2))
         add_record(2, 0, J)
         store_y(0, 3 * J)
-        for c in (VECTOR_CHUNK, 0, 1):
-            round_slot(2, c, nc.vector.tensor_copy)
-        for c in (2, SCALAR_LAST):
-            round_slot(2, c, nc.scalar.copy)
+        for a, b in [VECTOR_PIECE, (0, HALF)]:
+            round_slot(2, a, b, nc.vector.tensor_copy)
+        for a, b in [(HALF, VECTOR_PIECE[0]), SCALAR_PIECES[-1]]:
+            round_slot(2, a, b, nc.scalar.copy)
 
-        stored = 3 * J
-        for c, (a, b) in enumerate(CHUNKS):
+        for a, b in GATHERS:
             add_record(3, a, b)
-            if c != VECTOR_CHUNK:
-                round_slot(3, c, nc.scalar.copy)
-            if c in (2, VECTOR_CHUNK):
-                store_y(stored, 3 * J + b)
-                stored = 3 * J + b
+        for a, b in SCALAR_PIECES:
+            round_slot(3, a, b, nc.scalar.copy)
+        store_y(3 * J, 3 * J + GATHERS[3][0])
+        store_y(3 * J + GATHERS[3][0], 4 * J)
 
-        for c in (0, 1, 2):
-            quantise_chunk(c)
-        round_slot(3, VECTOR_CHUNK, nc.vector.tensor_copy)
-        for c in (SCALAR_LAST, VECTOR_CHUNK):
-            quantise_chunk(c)
-        for a, b in [(0, CHUNKS[2][1]), (CHUNKS[SCALAR_LAST][0], J)]:
-            nc.sync.dma_start(out=word_rows[:, a:b], in_=y_codes[:, a:b].bitcast(I32))
+        quantise(0, 256)
+        quantise(256, HALF)
+        store_words(0, HALF)
+        round_slot(3, *VECTOR_PIECE, nc.vector.tensor_copy)
+        quantise(HALF, VECTOR_PIECE[0])
+        quantise(*VECTOR_PIECE)
+        quantise(*SCALAR_PIECES[-1])
+        store_words(HALF, J)
         for r in range(4):
             queue = nc.sync if r % 2 == 0 else nc.scalar
             queue.dma_start(

@@ -195,8 +195,8 @@ def tile_list_engram_dl_sigLP_kernel(
         add_record(0, 0, J)
         add_record(1, 0, J)
         nc.scalar.copy(out=yb_slots[:, :, 0:2], in_=y[:, 0 : 2 * J].rearrange("p (e j) -> p j e", e=2))
+        store_y(0, 2 * J)
         add_record(2, 0, J)
-        store_y(0, 3 * J)
         for a, b in [VECTOR_PIECE, (0, HALF)]:
             round_slot(2, a, b, nc.vector.tensor_copy)
         for a, b in [(HALF, VECTOR_PIECE[0]), SCALAR_PIECES[-1]]:
@@ -206,8 +206,8 @@ def tile_list_engram_dl_sigLP_kernel(
             add_record(3, a, b)
         for a, b in SCALAR_PIECES:
             round_slot(3, a, b, nc.scalar.copy)
-        store_y(3 * J, 3 * J + GATHERS[3][0])
-        store_y(3 * J + GATHERS[3][0], 4 * J)
+        store_y(2 * J, 3 * J + GATHERS[1][1])
+        store_y(3 * J + GATHERS[1][1], 4 * J)
 
         quantise(0, 256)
         quantise(256, HALF)

@@ -44,16 +44,15 @@ def tile_list_engram_dl_sigLP_kernel(
         wk_raw = keep.tile([P, PACK, N], F32, name="wk_raw")
         wd_raw = keep.tile([P, PACK, N], F32, name="wd_raw")
         w4_raw = keep.tile([P, 2 * N], U8, name="w4_raw", align_bytes=64)
-        s4_raw = keep.tile([P, N], U8, name="s4_raw", align_bytes=64)
+        staged = keep.tile([P, J + N], U8, name="staged", align_bytes=64)
         st_pair = [keep.tile([P, 2 * J], F32, name="st%d" % u) for u in range(2)]
         st_sb = [st_pair[t // 2][:, (t % 2) * J : (t % 2 + 1) * J] for t in range(PACK)]
         r_sb = [keep.tile([P, T], F32, name="r%d" % t) for t in range(PACK)]
 
         planes = keep.tile([P, J + N], U8, name="planes", align_bytes=64)
         gs = planes[:, 0:J]
-        s4 = planes[:, J : J + N]
+        s4_raw = planes[:, J : J + N]
         nc.vector.memset(ts[:].bitcast(I32), 0)
-        nc.vector.memset(s4_raw[:].bitcast(I32), 0)
         nc.vector.memset(planes[:].bitcast(I32), 0)
 
         r_rows = rT.rearrange("(p t) c -> p t c", t=PACK)
@@ -63,18 +62,13 @@ def tile_list_engram_dl_sigLP_kernel(
         nc.sync.dma_start(offsets[:], offs)
         staged_rows = slice(STAGE_ROW, STAGE_ROW + 64, 4)
         nc.sync.dma_start(out=ts[staged_rows, :].bitcast(I32), in_=tab_scales[0].bitcast(I32))
-        nc.sync.dma_start(out=s4_raw[staged_rows, :].bitcast(I32), in_=wv4_scales[0].bitcast(I32))
+        nc.sync.dma_start(out=staged[staged_rows, J : J + N].bitcast(I32), in_=wv4_scales[0].bitcast(I32))
         nc.sync.dma_start(out=w4_raw[:].bitcast(I32), in_=wv4_words[0].bitcast(I32))
         nc.sync.dma_start(out=tw[:].bitcast(I32), in_=tab_words[0].rearrange("p t i -> p (t i)").bitcast(I32))
         nc.sync.dma_start(out=wd_raw[:], in_=wvd.rearrange("(p i) n -> p i n", i=PACK))
 
         picked = keep.tile([P, J], U8, name="picked", align_bytes=64)
         nc.vector.tensor_copy(picked[:], ts[:].indirect(offsets[:]))
-        staged = keep.tile([P, J + N], U8, name="staged", align_bytes=64)
-        nc.vector.tensor_copy(
-            out=staged[:, J : J + N].rearrange("p (t m) -> p m t", t=PACK),
-            in_=s4_raw[:].rearrange("p (m t) -> p m t", t=PACK),
-        )
         nc.vector.tensor_copy(out=staged[:, 0:J].bitcast(I32), in_=picked[:].bitcast(I32))
         for r in range(4):
             nc.sync.dma_start(
@@ -87,12 +81,15 @@ def tile_list_engram_dl_sigLP_kernel(
         for t in range(PACK):
             nc.sync.dma_start(out=r_sb[t][:], in_=r_rows[:, t, :])
 
-        def round_weight(raw, name):
+        def round_weight(raw, name, copies):
             grouped = keep.tile([P, PACK, P, PACK], BF16, name=name, align_bytes=64)
-            nc.scalar.copy(
-                out=grouped[:].rearrange("p t m i -> p m i t"),
-                in_=raw[:].rearrange("p i (m t) -> p m i t", t=PACK),
-            )
+            share = P // len(copies)
+            for c, copy in enumerate(copies):
+                ms = slice(c * share, (c + 1) * share)
+                copy(
+                    out=grouped[:].rearrange("p t m i -> p m i t")[:, ms],
+                    in_=raw[:].rearrange("p i (m t) -> p m i t", t=PACK)[:, ms],
+                )
             return grouped
 
         def quantise_weight(grouped, name):
@@ -103,17 +100,22 @@ def tile_list_engram_dl_sigLP_kernel(
             )
             return codes, scales
 
-        wk_grouped = round_weight(wk_raw, "wk_grouped")
+        wk_grouped = round_weight(wk_raw, "wk_grouped", [nc.scalar.copy])
         wk_codes, wk_scales = quantise_weight(wk_grouped, "wk")
         w4 = keep.tile([P, 2 * N], U8, name="w4", align_bytes=64)
         nc.vector.tensor_copy(
-            out=w4[:].rearrange("p (t m b) -> p m t b", t=PACK, b=2),
-            in_=w4_raw[:].rearrange("p (m t b) -> p m t b", t=PACK, b=2),
+            out=w4[:].rearrange("p (t m b) -> p t m b", t=PACK, b=2),
+            in_=w4_raw[:].rearrange("p (m t b) -> p t m b", t=PACK, b=2),
         )
         gw = [keep.tile([P, HALF], U32, name="gw%d" % h, align_bytes=64) for h in range(2)]
         for h in range(2):
             nc.vector.tensor_copy(gw[h][:], tw[:].indirect(offsets[:, h * HALF // 16 : (h + 1) * HALF // 16]))
-        wd_codes, wd_scales = quantise_weight(round_weight(wd_raw, "wd_grouped"), "wd")
+        wd_grouped = round_weight(wd_raw, "wd_grouped", [nc.scalar.copy, nc.vector.tensor_copy])
+        s4 = keep.tile([P, N], U8, name="s4", align_bytes=64)
+        nc.vector.tensor_copy(
+            out=s4[:].rearrange("p (t m) -> p t m", t=PACK), in_=s4_raw.rearrange("p (m t) -> p t m", t=PACK)
+        )
+        wd_codes, wd_scales = quantise_weight(wd_grouped, "wd")
 
         gv = [keep.tile([P, J], F32, name="gv%d" % t) for t in range(PACK)]
         gates = {}

@@ -19,6 +19,7 @@ SIGMOID = mybir.ActivationFunctionType.Sigmoid
 
 P = 128
 PACK = 4
+BURST = 256
 HALF = 512
 
 GATHERS = [(0, 128), (128, 320), (320, 608), (608, 1024)]
@@ -38,18 +39,18 @@ def tile_list_engram_dl_sigLP_kernel(
         ring = ctx.enter_context(tc.tile_pool(name="ring", bufs=8))
         psum = ctx.enter_context(tc.psum_pool(name="psum", bufs=4))
 
-        offsets = keep.tile([P, J // 16], U16, name="offsets")
-        tw = keep.tile([P, T], U32, name="tw", align_bytes=64)
-        ts = keep.tile([P, T], U8, name="ts", align_bytes=64)
-        wk_raw = keep.tile([P, PACK, N], F32, name="wk_raw")
-        wd_raw = keep.tile([P, PACK, N], F32, name="wd_raw")
-        w4_raw = keep.tile([P, 2 * N], U8, name="w4_raw", align_bytes=64)
-        staged = keep.tile([P, J + N], U8, name="staged", align_bytes=64)
-        st_pair = [keep.tile([P, 2 * J], F32, name="st%d" % u) for u in range(2)]
+        offsets = keep.tile([P, J // 16], U16, name="offsets", align_bytes=BURST)
+        tw = keep.tile([P, T], U32, name="tw", align_bytes=BURST)
+        ts = keep.tile([P, T], U8, name="ts", align_bytes=BURST)
+        wk_raw = keep.tile([P, PACK, N], F32, name="wk_raw", align_bytes=BURST)
+        wd_raw = keep.tile([P, PACK, N], F32, name="wd_raw", align_bytes=BURST)
+        w4_raw = keep.tile([P, 2 * N], U8, name="w4_raw", align_bytes=BURST)
+        staged = keep.tile([P, J + N], U8, name="staged", align_bytes=BURST)
+        st_pair = [keep.tile([P, 2 * J], F32, name="st%d" % u, align_bytes=BURST) for u in range(2)]
         st_sb = [st_pair[t // 2][:, (t % 2) * J : (t % 2 + 1) * J] for t in range(PACK)]
-        r_sb = [keep.tile([P, T], F32, name="r%d" % t) for t in range(PACK)]
+        r_sb = [keep.tile([P, T], F32, name="r%d" % t, align_bytes=BURST) for t in range(PACK)]
 
-        planes = keep.tile([P, J + N], U8, name="planes", align_bytes=64)
+        planes = keep.tile([P, J + N], U8, name="planes", align_bytes=BURST)
         gs = planes[:, 0:J]
         s4_raw = planes[:, J : J + N]
         nc.vector.memset(ts[:].bitcast(I32), 0)
@@ -167,11 +168,11 @@ def tile_list_engram_dl_sigLP_kernel(
             for h in range(2):
                 make_value(t, h)
 
-        y = keep.tile([P, PACK * J], F32, name="y")
+        y = keep.tile([P, PACK * J], F32, name="y", align_bytes=BURST)
         yb = keep.tile([P, J * PACK], BF16, name="yb", align_bytes=64)
         yb_slots = yb[:].rearrange("p (j t) -> p j t", t=PACK)
-        y_codes = keep.tile([P, J], U32, name="y_codes", align_bytes=64)
-        y_scales = keep.tile([P, J], U8, name="y_scales", align_bytes=64)
+        y_codes = keep.tile([P, J], U32, name="y_codes", align_bytes=BURST)
+        y_scales = keep.tile([P, J], U8, name="y_scales", align_bytes=BURST)
         y_rows = out_0.rearrange("(p t) j -> p (t j)", t=PACK)
         word_rows = out_1[0].rearrange("p j i -> p (j i)").bitcast(I32)
 

@@ -20,6 +20,7 @@ SIGMOID = mybir.ActivationFunctionType.Sigmoid
 P = 128
 PACK = 4
 BURST = 256
+PAGE = 4096
 HALF = 512
 
 GATHERS = [(0, 128), (128, 320), (320, 608), (608, 1024)]
@@ -36,19 +37,26 @@ def tile_list_engram_dl_sigLP_kernel(
     nc = tc.nc
     with ExitStack() as ctx:
         keep = ctx.enter_context(tc.tile_pool(name="keep", bufs=1))
+        paged = ctx.enter_context(tc.tile_pool(name="paged", bufs=1))
+        taken = [0]
+
+        def paged_tile(shape, dtype, name, pages):
+            taken.append(taken[-1] + pages * PAGE)
+            return paged.tile(shape, dtype, name=name, offset=taken[-2], align_bytes=PAGE)
+
         ring = ctx.enter_context(tc.tile_pool(name="ring", bufs=8))
         psum = ctx.enter_context(tc.psum_pool(name="psum", bufs=4))
 
         offsets = keep.tile([P, J // 16], U16, name="offsets", align_bytes=BURST)
-        tw = keep.tile([P, T], U32, name="tw", align_bytes=BURST)
-        ts = keep.tile([P, T], U8, name="ts", align_bytes=BURST)
-        wk_raw = keep.tile([P, PACK, N], F32, name="wk_raw", align_bytes=BURST)
-        wd_raw = keep.tile([P, PACK, N], F32, name="wd_raw", align_bytes=BURST)
+        tw = paged_tile([P, T], U32, "tw", 4)
+        ts = paged_tile([P, T], U8, "ts", 1)
+        wk_raw = paged_tile([P, PACK, N], F32, "wk_raw", 2)
+        wd_raw = paged_tile([P, PACK, N], F32, "wd_raw", 2)
         w4_raw = keep.tile([P, 2 * N], U8, name="w4_raw", align_bytes=BURST)
         staged = keep.tile([P, J + N], U8, name="staged", align_bytes=BURST)
-        st_pair = [keep.tile([P, 2 * J], F32, name="st%d" % u, align_bytes=BURST) for u in range(2)]
+        st_pair = [paged_tile([P, 2 * J], F32, "st%d" % u, 2) for u in range(2)]
         st_sb = [st_pair[t // 2][:, (t % 2) * J : (t % 2 + 1) * J] for t in range(PACK)]
-        r_sb = [keep.tile([P, T], F32, name="r%d" % t, align_bytes=BURST) for t in range(PACK)]
+        r_sb = [paged_tile([P, T], F32, "r%d" % t, 4) for t in range(PACK)]
 
         planes = keep.tile([P, J + N], U8, name="planes", align_bytes=BURST)
         gs = planes[:, 0:J]
@@ -168,10 +176,10 @@ def tile_list_engram_dl_sigLP_kernel(
             for h in range(2):
                 make_value(t, h)
 
-        y = keep.tile([P, PACK * J], F32, name="y", align_bytes=BURST)
+        y = paged_tile([P, PACK * J], F32, "y", 4)
         yb = keep.tile([P, J * PACK], BF16, name="yb", align_bytes=64)
         yb_slots = yb[:].rearrange("p (j t) -> p j t", t=PACK)
-        y_codes = keep.tile([P, J], U32, name="y_codes", align_bytes=BURST)
+        y_codes = paged_tile([P, J], U32, "y_codes", 1)
         y_scales = keep.tile([P, J], U8, name="y_scales", align_bytes=BURST)
         y_rows = out_0.rearrange("(p t) j -> p (t j)", t=PACK)
         word_rows = out_1[0].rearrange("p j i -> p (j i)").bitcast(I32)

@@ -23,9 +23,9 @@ BURST = 256
 PAGE = 4096
 HALF = 512
 
-GATHERS = [(0, 128), (128, 320), (320, 608), (608, 1024)]
+GATHERS = [(0, 128), (128, 320), (320, 512), (512, 768), (768, 1024)]
 VECTOR_PIECE = (768, 896)
-SCALAR_PIECES = GATHERS[:3] + [(608, 768), (896, 1024)]
+SCALAR_PIECES = GATHERS[:4] + [(896, 1024)]
 
 STAGE_ROW = 32
 OUT_PLANE = 8

@@ -25,7 +25,8 @@ HALF = 512
 
 GATHERS = [(0, 128), (128, 320), (320, 512), (512, 768), (768, 1024)]
 VECTOR_PIECE = (768, 896)
-SCALAR_PIECES = GATHERS[:4] + [(896, 1024)]
+SCALAR_PIECES = GATHERS[:3] + [(512, 640), (640, 768), (896, 1024)]
+WORD_CUT = 640
 
 STAGE_ROW = 32
 OUT_PLANE = 8
@@ -206,8 +207,8 @@ def tile_list_engram_dl_sigLP_kernel(
         add_record(0, 0, J)
         add_record(1, 0, J)
         nc.scalar.copy(out=yb_slots[:, :, 0:2], in_=y[:, 0 : 2 * J].rearrange("p (e j) -> p j e", e=2))
-        store_y(0, 2 * J)
         add_record(2, 0, J)
+        store_y(0, 2 * J + HALF)
         for a, b in [VECTOR_PIECE, (0, HALF)]:
             round_slot(2, a, b, nc.vector.tensor_copy)
         for a, b in [(HALF, VECTOR_PIECE[0]), SCALAR_PIECES[-1]]:
@@ -217,17 +218,18 @@ def tile_list_engram_dl_sigLP_kernel(
             add_record(3, a, b)
         for a, b in SCALAR_PIECES:
             round_slot(3, a, b, nc.scalar.copy)
-        store_y(2 * J, 3 * J + GATHERS[1][1])
-        store_y(3 * J + GATHERS[1][1], 4 * J)
+        store_y(2 * J + HALF, 3 * J + HALF)
+        store_y(3 * J + HALF, 4 * J)
 
         quantise(0, 256)
         quantise(256, HALF)
-        store_words(0, HALF)
+        quantise(HALF, WORD_CUT)
+        store_words(0, WORD_CUT)
         round_slot(3, *VECTOR_PIECE, nc.vector.tensor_copy)
-        quantise(HALF, VECTOR_PIECE[0])
+        quantise(WORD_CUT, VECTOR_PIECE[0])
         quantise(*VECTOR_PIECE)
         quantise(*SCALAR_PIECES[-1])
-        store_words(HALF, J)
+        store_words(WORD_CUT, J)
         for r in range(4):
             queue = nc.sync if r % 2 == 0 else nc.scalar
             queue.dma_start(

@@ -26,6 +26,7 @@ HALF = 512
 GATHERS = [(0, 128), (128, 320), (320, 512), (512, 768), (768, 1024)]
 VECTOR_PIECE = (768, 896)
 SCALAR_PIECES = GATHERS[:3] + [(512, 640), (640, 768), (896, 1024)]
+THIRD_GATHERS = [(0, 256), (256, 640), (640, 1024)]
 WORD_CUT = 640
 
 STAGE_ROW = 32
@@ -46,7 +47,7 @@ def tile_list_engram_dl_sigLP_kernel(
             return paged.tile(shape, dtype, name=name, offset=taken[-2], align_bytes=PAGE)
 
         ring = ctx.enter_context(tc.tile_pool(name="ring", bufs=8))
-        psum = ctx.enter_context(tc.psum_pool(name="psum", bufs=4))
+        psum = ctx.enter_context(tc.psum_pool(name="psum", bufs=8))
 
         offsets = keep.tile([P, J // 16], U16, name="offsets", align_bytes=BURST)
         tw = paged_tile([P, T], U32, "tw", 4)
@@ -54,16 +55,20 @@ def tile_list_engram_dl_sigLP_kernel(
         wk_raw = paged_tile([P, PACK, N], F32, "wk_raw", 2)
         wd_raw = paged_tile([P, PACK, N], F32, "wd_raw", 2)
         w4_raw = keep.tile([P, 2 * N], U8, name="w4_raw", align_bytes=BURST)
-        staged = keep.tile([P, J + N], U8, name="staged", align_bytes=BURST)
-        st_pair = [paged_tile([P, 2 * J], F32, "st%d" % u, 2) for u in range(2)]
-        st_sb = [st_pair[t // 2][:, (t % 2) * J : (t % 2 + 1) * J] for t in range(PACK)]
+        st_all = paged_tile([P, PACK * J], F32, "st_all", 4)
+        st_sb = [st_all[:, t * J : (t + 1) * J] for t in range(PACK)]
         r_sb = [paged_tile([P, T], F32, "r%d" % t, 4) for t in range(PACK)]
 
-        planes = keep.tile([P, J + N], U8, name="planes", align_bytes=BURST)
-        gs = planes[:, 0:J]
-        s4_raw = planes[:, J : J + N]
+        gs = keep.tile([P, J], U8, name="gs", align_bytes=BURST)
+        s4_raw = keep.tile([P, N], U8, name="s4_raw", align_bytes=BURST)
         nc.vector.memset(ts[:].bitcast(I32), 0)
-        nc.vector.memset(planes[:].bitcast(I32), 0)
+        nc.vector.memset(gs[:].bitcast(I32), 0)
+        nc.gpsimd.memset(s4_raw[:].bitcast(I32), 0)
+
+        for r in range(4):
+            nc.gpsimd.dma_start(
+                out=s4_raw[r:P:32, :].bitcast(I32), in_=wv4_scales[0, r:16:4, :].bitcast(I32), max_dma_last_dim=N // 2
+            )
 
         r_rows = rT.rearrange("(p t) c -> p t c", t=PACK)
         st_rows = st.rearrange("(p t) j -> p (t j)", t=PACK)
@@ -72,22 +77,19 @@ def tile_list_engram_dl_sigLP_kernel(
         nc.sync.dma_start(offsets[:], offs)
         staged_rows = slice(STAGE_ROW, STAGE_ROW + 64, 4)
         nc.sync.dma_start(out=ts[staged_rows, :].bitcast(I32), in_=tab_scales[0].bitcast(I32))
-        nc.sync.dma_start(out=staged[staged_rows, J : J + N].bitcast(I32), in_=wv4_scales[0].bitcast(I32))
         nc.sync.dma_start(out=w4_raw[:].bitcast(I32), in_=wv4_words[0].bitcast(I32))
         nc.sync.dma_start(out=tw[:].bitcast(I32), in_=tab_words[0].rearrange("p t i -> p (t i)").bitcast(I32))
         nc.sync.dma_start(out=wd_raw[:], in_=wvd.rearrange("(p i) n -> p i n", i=PACK))
 
-        picked = keep.tile([P, J], U8, name="picked", align_bytes=64)
+        picked = keep.tile([P, J], U8, name="picked", align_bytes=BURST)
         nc.vector.tensor_copy(picked[:], ts[:].indirect(offsets[:]))
-        nc.vector.tensor_copy(out=staged[:, 0:J].bitcast(I32), in_=picked[:].bitcast(I32))
         for r in range(4):
             nc.sync.dma_start(
-                out=planes[r:P:32, :].bitcast(I32),
-                in_=staged[STAGE_ROW + 4 * r : STAGE_ROW + 64 : 16, :].bitcast(I32),
+                out=gs[r:P:32, :].bitcast(I32),
+                in_=picked[STAGE_ROW + 4 * r : STAGE_ROW + 64 : 16, :].bitcast(I32),
             )
 
-        for u in range(2):
-            nc.sync.dma_start(out=st_pair[u][:], in_=st_rows[:, 2 * u * J : 2 * (u + 1) * J])
+        nc.sync.dma_start(out=st_all[:], in_=st_rows)
         for t in range(PACK):
             nc.sync.dma_start(out=r_sb[t][:], in_=r_rows[:, t, :])
 
@@ -121,61 +123,57 @@ def tile_list_engram_dl_sigLP_kernel(
         for h in range(2):
             nc.vector.tensor_copy(gw[h][:], tw[:].indirect(offsets[:, h * HALF // 16 : (h + 1) * HALF // 16]))
         wd_grouped = round_weight(wd_raw, "wd_grouped", [nc.scalar.copy, nc.vector.tensor_copy])
-        s4 = keep.tile([P, N], U8, name="s4", align_bytes=64)
+        s4 = paged.tile([P, N], U8, name="s4", offset=0, align_bytes=PAGE)
         nc.vector.tensor_copy(
-            out=s4[:].rearrange("p (t m) -> p t m", t=PACK), in_=s4_raw.rearrange("p (m t) -> p t m", t=PACK)
+            out=s4[:].rearrange("p (t m) -> p t m", t=PACK), in_=s4_raw[:].rearrange("p (m t) -> p t m", t=PACK)
         )
         wd_codes, wd_scales = quantise_weight(wd_grouped, "wd")
 
         gv = [keep.tile([P, J], F32, name="gv%d" % t) for t in range(PACK)]
-        gates = {}
 
-        def make_key(t, h):
+        def product(t, h, weights):
             cols = slice(h * HALF, (h + 1) * HALF)
-            ms = slice(t * P, (t + 1) * P)
-            ke = psum.tile([P, HALF], F32, name="ke")
-            nc.tensor.matmul_mx(
-                out=ke[:], lhsT=wk_codes[:, ms].bitcast(FP8X4), lhsT_scale=wk_scales[:, ms],
-                rhs=gw[h][:].bitcast(FP8X4), rhs_scale=gs[:, cols], start=True, stop=True,
-            )
-            return ke
+            bank = psum.tile([P, HALF], F32, name="bank")
+            for i, (codes, scales) in enumerate(weights):
+                nc.tensor.matmul_mx(
+                    out=bank[:], lhsT=codes, lhsT_scale=scales, rhs=gw[h][:].bitcast(FP8X4), rhs_scale=gs[:, cols],
+                    start=i == 0, stop=i == len(weights) - 1,
+                )
+            return bank
 
-        def make_gate(t, h, ke, engine):
+        def key(t, h):
+            ms = slice(t * P, (t + 1) * P)
+            return product(t, h, [(wk_codes[:, ms].bitcast(FP8X4), wk_scales[:, ms])])
+
+        def value(t, h):
+            ms = slice(t * P, (t + 1) * P)
+            base = (w4[:, 2 * t * P : 2 * (t + 1) * P].bitcast(FP4X4), s4[:, ms])
+            return product(t, h, [base, (wd_codes[:, ms].bitcast(FP8X4), wd_scales[:, ms])])
+
+        def gate(t, h, ke, engine):
             z = ring.tile([P, HALF], F32, name="z")
             engine.tensor_tensor(z[:], ke[:], st_sb[t][:, h * HALF : (h + 1) * HALF], MULT)
-            gate = ring.tile([P, HALF], F32, name="gate")
-            nc.scalar.activation(gate[:], z[:], SIGMOID)
-            gates[(t, h)] = gate
+            g = ring.tile([P, HALF], F32, name="g")
+            nc.scalar.activation(g[:], z[:], SIGMOID)
+            return g
 
-        def make_value(t, h):
-            cols = slice(h * HALF, (h + 1) * HALF)
-            ms = slice(t * P, (t + 1) * P)
-            ve = psum.tile([P, HALF], F32, name="ve")
-            nc.tensor.matmul_mx(
-                out=ve[:], lhsT=w4[:, 2 * t * P : 2 * (t + 1) * P].bitcast(FP4X4), lhsT_scale=s4[:, ms],
-                rhs=gw[h][:].bitcast(FP8X4), rhs_scale=gs[:, cols], start=True, stop=False,
-            )
-            nc.tensor.matmul_mx(
-                out=ve[:], lhsT=wd_codes[:, ms].bitcast(FP8X4), lhsT_scale=wd_scales[:, ms],
-                rhs=gw[h][:].bitcast(FP8X4), rhs_scale=gs[:, cols], start=False, stop=True,
-            )
-            nc.vector.tensor_tensor(gv[t][:, cols], ve[:], gates[(t, h)][:], MULT)
+        def let_through(t, h, ve, g):
+            nc.vector.tensor_tensor(gv[t][:, h * HALF : (h + 1) * HALF], ve[:], g[:], MULT)
 
-        ke_sb = [keep.tile([P, HALF], F32, name="ke_sb%d" % h) for h in range(2)]
-        for h in range(2):
-            nc.scalar.copy(out=ke_sb[h][:], in_=make_key(3, h)[:])
-        for t in range(2):
-            for h in range(2):
-                make_gate(t, h, make_key(t, h), nc.vector)
-        for t in range(2):
-            for h in range(2):
-                make_value(t, h)
-        for h in range(2):
-            make_gate(3, h, ke_sb[h], nc.gpsimd)
-            make_gate(2, h, make_key(2, h), nc.vector)
-        for t in (2, 3):
-            for h in range(2):
-                make_value(t, h)
+        early = [(t, h) for t in (0, 1) for h in range(2)]
+        late = [(t, h) for t in (2, 3) for h in range(2)]
+        keys = {}
+        for t, h in late:
+            keys[(t, h)] = keep.tile([P, HALF], F32, name="parked%d%d" % (t, h))
+            nc.scalar.copy(out=keys[(t, h)][:], in_=key(t, h)[:])
+        for t, h in early:
+            keys[(t, h)] = key(t, h)
+        values = {th: value(*th) for th in early}
+        gates = {th: gate(*th, keys[th], nc.vector) for th in early}
+        gates.update({th: gate(*th, keys[th], nc.gpsimd) for th in late})
+        values.update({th: value(*th) for th in late})
+        for th in early + late:
+            let_through(*th, values[th], gates[th])
 
         y = paged_tile([P, PACK * J], F32, "y", 4)
         yb = keep.tile([P, J * PACK], BF16, name="yb", align_bytes=64)
@@ -204,15 +202,20 @@ def tile_list_engram_dl_sigLP_kernel(
         def store_y(a, b):
             nc.sync.dma_start(out=y_rows[:, a:b], in_=y[:, a:b])
 
+        def round_pair(a, b, copy):
+            copy(out=yb_slots[:, a:b, 0:2], in_=y[:, 0 : 2 * J].rearrange("p (e j) -> p j e", e=2)[:, a:b])
+
         add_record(0, 0, J)
-        add_record(1, 0, J)
-        nc.scalar.copy(out=yb_slots[:, :, 0:2], in_=y[:, 0 : 2 * J].rearrange("p (e j) -> p j e", e=2))
-        add_record(2, 0, J)
+        add_record(1, 0, HALF)
+        add_record(1, HALF, J)
+        round_pair(0, HALF, nc.scalar.copy)
+        round_pair(HALF, J, nc.vector.tensor_copy)
+        for a, b in THIRD_GATHERS:
+            add_record(2, a, b)
         store_y(0, 2 * J + HALF)
-        for a, b in [VECTOR_PIECE, (0, HALF)]:
-            round_slot(2, a, b, nc.vector.tensor_copy)
-        for a, b in [(HALF, VECTOR_PIECE[0]), SCALAR_PIECES[-1]]:
+        for a, b in THIRD_GATHERS[:2]:
             round_slot(2, a, b, nc.scalar.copy)
+        round_slot(2, *THIRD_GATHERS[2], nc.vector.tensor_copy)
 
         for a, b in GATHERS:
             add_record(3, a, b)

@@ -26,10 +26,8 @@ HALF = 512
 GATHERS = [(0, 128), (128, 320), (320, 512), (512, 768), (768, 1024)]
 VECTOR_PIECE = (768, 896)
 SCALAR_PIECES = GATHERS[:3] + [(512, 640), (640, 768), (896, 1024)]
-THIRD_GATHERS = [(0, 256), (256, 640), (640, 1024)]
 WORD_CUT = 640
 
-STAGE_ROW = 32
 OUT_PLANE = 8
 
 
@@ -59,35 +57,29 @@ def tile_list_engram_dl_sigLP_kernel(
         st_sb = [st_all[:, t * J : (t + 1) * J] for t in range(PACK)]
         r_sb = [paged_tile([P, T], F32, "r%d" % t, 4) for t in range(PACK)]
 
-        gs = keep.tile([P, J], U8, name="gs", align_bytes=BURST)
-        s4_raw = keep.tile([P, N], U8, name="s4_raw", align_bytes=BURST)
+        planes = keep.tile([P, J + N], U8, name="planes", align_bytes=BURST)
+        gs = planes[:, 0:J]
+        s4_raw = planes[:, J : J + N]
         nc.vector.memset(ts[:].bitcast(I32), 0)
-        nc.vector.memset(gs[:].bitcast(I32), 0)
-        nc.gpsimd.memset(s4_raw[:].bitcast(I32), 0)
-
-        for r in range(4):
-            nc.gpsimd.dma_start(
-                out=s4_raw[r:P:32, :].bitcast(I32), in_=wv4_scales[0, r:16:4, :].bitcast(I32), max_dma_last_dim=N // 2
-            )
+        nc.vector.memset(s4_raw.bitcast(I32), 0)
 
         r_rows = rT.rearrange("(p t) c -> p t c", t=PACK)
         st_rows = st.rearrange("(p t) j -> p (t j)", t=PACK)
 
         nc.sync.dma_start(out=wk_raw[:], in_=wk.rearrange("(p i) n -> p i n", i=PACK))
         nc.sync.dma_start(offsets[:], offs)
-        staged_rows = slice(STAGE_ROW, STAGE_ROW + 64, 4)
+        staged_rows = slice(0, P, 8)
         nc.sync.dma_start(out=ts[staged_rows, :].bitcast(I32), in_=tab_scales[0].bitcast(I32))
+        nc.sync.dma_start(out=planes[staged_rows, J : J + N].bitcast(I32), in_=wv4_scales[0].bitcast(I32))
         nc.sync.dma_start(out=w4_raw[:].bitcast(I32), in_=wv4_words[0].bitcast(I32))
         nc.sync.dma_start(out=tw[:].bitcast(I32), in_=tab_words[0].rearrange("p t i -> p (t i)").bitcast(I32))
         nc.sync.dma_start(out=wd_raw[:], in_=wvd.rearrange("(p i) n -> p i n", i=PACK))
 
-        picked = keep.tile([P, J], U8, name="picked", align_bytes=BURST)
+        picked = keep.tile([P, J], U8, name="picked", align_bytes=64)
         nc.vector.tensor_copy(picked[:], ts[:].indirect(offsets[:]))
-        for r in range(4):
-            nc.sync.dma_start(
-                out=gs[r:P:32, :].bitcast(I32),
-                in_=picked[STAGE_ROW + 4 * r : STAGE_ROW + 64 : 16, :].bitcast(I32),
-            )
+        nc.vector.tensor_copy(out=gs.bitcast(I32), in_=picked[:].bitcast(I32))
+        for r in range(1, 4):
+            nc.sync.dma_start(out=planes[r:P:32, :].bitcast(I32), in_=planes[8 * r : P : 32, :].bitcast(I32))
 
         nc.sync.dma_start(out=st_all[:], in_=st_rows)
         for t in range(PACK):
@@ -123,9 +115,9 @@ def tile_list_engram_dl_sigLP_kernel(
         for h in range(2):
             nc.vector.tensor_copy(gw[h][:], tw[:].indirect(offsets[:, h * HALF // 16 : (h + 1) * HALF // 16]))
         wd_grouped = round_weight(wd_raw, "wd_grouped", [nc.scalar.copy, nc.vector.tensor_copy])
-        s4 = paged.tile([P, N], U8, name="s4", offset=0, align_bytes=PAGE)
+        s4 = keep.tile([P, N], U8, name="s4", align_bytes=64)
         nc.vector.tensor_copy(
-            out=s4[:].rearrange("p (t m) -> p t m", t=PACK), in_=s4_raw[:].rearrange("p (m t) -> p t m", t=PACK)
+            out=s4[:].rearrange("p (t m) -> p t m", t=PACK), in_=s4_raw.rearrange("p (m t) -> p t m", t=PACK)
         )
         wd_codes, wd_scales = quantise_weight(wd_grouped, "wd")
 
@@ -162,9 +154,12 @@ def tile_list_engram_dl_sigLP_kernel(
 
         early = [(t, h) for t in (0, 1) for h in range(2)]
         late = [(t, h) for t in (2, 3) for h in range(2)]
+        y_offset = taken[-1]
         keys = {}
         for t, h in late:
-            keys[(t, h)] = keep.tile([P, HALF], F32, name="parked%d%d" % (t, h))
+            keys[(t, h)] = paged.tile(
+                [P, HALF], F32, name="parked%d%d" % (t, h), offset=y_offset + len(keys) * 4 * HALF, align_bytes=BURST
+            )
             nc.scalar.copy(out=keys[(t, h)][:], in_=key(t, h)[:])
         for t, h in early:
             keys[(t, h)] = key(t, h)
@@ -202,20 +197,18 @@ def tile_list_engram_dl_sigLP_kernel(
         def store_y(a, b):
             nc.sync.dma_start(out=y_rows[:, a:b], in_=y[:, a:b])
 
-        def round_pair(a, b, copy):
-            copy(out=yb_slots[:, a:b, 0:2], in_=y[:, 0 : 2 * J].rearrange("p (e j) -> p j e", e=2)[:, a:b])
+        def round_pair(a, b):
+            nc.scalar.copy(out=yb_slots[:, a:b, 0:2], in_=y[:, 0 : 2 * J].rearrange("p (e j) -> p j e", e=2)[:, a:b])
 
-        add_record(0, 0, J)
-        add_record(1, 0, HALF)
-        add_record(1, HALF, J)
-        round_pair(0, HALF, nc.scalar.copy)
-        round_pair(HALF, J, nc.vector.tensor_copy)
-        for a, b in THIRD_GATHERS:
-            add_record(2, a, b)
+        for a in (0, HALF):
+            add_record(0, a, a + HALF)
+            add_record(1, a, a + HALF)
+            round_pair(a, a + HALF)
+        add_record(2, 0, HALF)
+        add_record(2, HALF, J)
         store_y(0, 2 * J + HALF)
-        for a, b in THIRD_GATHERS[:2]:
-            round_slot(2, a, b, nc.scalar.copy)
-        round_slot(2, *THIRD_GATHERS[2], nc.vector.tensor_copy)
+        round_slot(2, 0, HALF, nc.scalar.copy)
+        round_slot(2, HALF, J, nc.vector.tensor_copy)
 
         for a, b in GATHERS:
             add_record(3, a, b)

@@ -161,9 +161,11 @@ def tile_list_engram_dl_sigLP_kernel(
                 [P, HALF], F32, name="parked%d%d" % (t, h), offset=y_offset + len(keys) * 4 * HALF, align_bytes=BURST
             )
             nc.scalar.copy(out=keys[(t, h)][:], in_=key(t, h)[:])
-        for t, h in early:
-            keys[(t, h)] = key(t, h)
-        values = {th: value(*th) for th in early}
+        for th in early[:-1]:
+            keys[th] = key(*th)
+        values = {early[0]: value(*early[0])}
+        keys[early[-1]] = key(*early[-1])
+        values.update({th: value(*th) for th in early[1:]})
         gates = {th: gate(*th, keys[th], nc.vector) for th in early}
         gates.update({th: gate(*th, keys[th], nc.gpsimd) for th in late})
         values.update({th: value(*th) for th in late})
@@ -200,8 +202,8 @@ def tile_list_engram_dl_sigLP_kernel(
         def round_pair(a, b):
             nc.scalar.copy(out=yb_slots[:, a:b, 0:2], in_=y[:, 0 : 2 * J].rearrange("p (e j) -> p j e", e=2)[:, a:b])
 
+        add_record(0, 0, J)
         for a in (0, HALF):
-            add_record(0, a, a + HALF)
             add_record(1, a, a + HALF)
             round_pair(a, a + HALF)
         add_record(2, 0, HALF)

@@ -25,8 +25,7 @@ HALF = 512
 
 GATHERS = [(0, 128), (128, 320), (320, 512), (512, 768), (768, 1024)]
 VECTOR_PIECE = (768, 896)
-SCALAR_PIECES = GATHERS[:3] + [(512, 640), (640, 768), (896, 1024)]
-WORD_CUT = 640
+SCALAR_PIECES = GATHERS[:4] + [(896, 1024)]
 
 OUT_PLANE = 8
 
@@ -202,8 +201,8 @@ def tile_list_engram_dl_sigLP_kernel(
         def round_pair(a, b):
             nc.scalar.copy(out=yb_slots[:, a:b, 0:2], in_=y[:, 0 : 2 * J].rearrange("p (e j) -> p j e", e=2)[:, a:b])
 
-        add_record(0, 0, J)
         for a in (0, HALF):
+            add_record(0, a, a + HALF)
             add_record(1, a, a + HALF)
             round_pair(a, a + HALF)
         add_record(2, 0, HALF)
@@ -221,13 +220,13 @@ def tile_list_engram_dl_sigLP_kernel(
 
         quantise(0, 256)
         quantise(256, HALF)
-        quantise(HALF, WORD_CUT)
-        store_words(0, WORD_CUT)
+        store_words(0, HALF)
         round_slot(3, *VECTOR_PIECE, nc.vector.tensor_copy)
-        quantise(WORD_CUT, VECTOR_PIECE[0])
+        quantise(HALF, VECTOR_PIECE[0])
+        store_words(HALF, VECTOR_PIECE[0])
         quantise(*VECTOR_PIECE)
         quantise(*SCALAR_PIECES[-1])
-        store_words(WORD_CUT, J)
+        store_words(VECTOR_PIECE[0], J)
         for r in range(4):
             queue = nc.sync if r % 2 == 0 else nc.scalar
             queue.dma_start(

@@ -113,7 +113,7 @@ def tile_list_engram_dl_sigLP_kernel(
         gw = [keep.tile([P, HALF], U32, name="gw%d" % h, align_bytes=64) for h in range(2)]
         for h in range(2):
             nc.vector.tensor_copy(gw[h][:], tw[:].indirect(offsets[:, h * HALF // 16 : (h + 1) * HALF // 16]))
-        wd_grouped = round_weight(wd_raw, "wd_grouped", [nc.scalar.copy, nc.vector.tensor_copy])
+        wd_grouped = round_weight(wd_raw, "wd_grouped", [nc.scalar.copy])
         s4 = keep.tile([P, N], U8, name="s4", align_bytes=64)
         nc.vector.tensor_copy(
             out=s4[:].rearrange("p (t m) -> p t m", t=PACK), in_=s4_raw.rearrange("p (m t) -> p t m", t=PACK)

from contextlib import ExitStack

import concourse.mybir as mybir

K, N, T, J = 512, 512, 4096, 1024
FLOPS = 3 * 2 * K * N * J

F32 = mybir.dt.float32
BF16 = mybir.dt.bfloat16
I32 = mybir.dt.int32
U32 = mybir.dt.uint32
U16 = mybir.dt.uint16
U8 = mybir.dt.uint8
FP8X4 = mybir.dt.float8_e4m3fn_x4
FP4X4 = mybir.dt.float4_e2m1fn_x4
MULT = mybir.AluOpType.mult
ADD = mybir.AluOpType.add
SIGMOID = mybir.ActivationFunctionType.Sigmoid

P = 128
PACK = 4
BURST = 256
PAGE = 4096
HALF = 512

GATHERS = [(0, 128), (128, 320), (320, 512), (512, 768), (768, 1024)]
VECTOR_PIECE = (768, 896)
SCALAR_PIECES = GATHERS[:4] + [(896, 1024)]

OUT_PLANE = 8


def tile_list_engram_dl_sigLP_kernel(
    tc, tab_words, tab_scales, wk, wv4_words, wv4_scales, wvd, st, rT, offs, out_0, out_1, out_2
):
    nc = tc.nc
    with ExitStack() as ctx:
        keep = ctx.enter_context(tc.tile_pool(name="keep", bufs=1))
        paged = ctx.enter_context(tc.tile_pool(name="paged", bufs=1))
        taken = [0]

        def paged_tile(shape, dtype, name, pages):
            taken.append(taken[-1] + pages * PAGE)
            return paged.tile(shape, dtype, name=name, offset=taken[-2], align_bytes=PAGE)

        ring = ctx.enter_context(tc.tile_pool(name="ring", bufs=8))
        psum = ctx.enter_context(tc.psum_pool(name="psum", bufs=8))

        offsets = keep.tile([P, J // 16], U16, name="offsets", align_bytes=BURST)
        tw = paged_tile([P, T], U32, "tw", 4)
        ts = paged_tile([P, T], U8, "ts", 1)
        wk_raw = paged_tile([P, PACK, N], F32, "wk_raw", 2)
        wd_raw = paged_tile([P, PACK, N], F32, "wd_raw", 2)
        w4_raw = keep.tile([P, 2 * N], U8, name="w4_raw", align_bytes=BURST)
        st_all = paged_tile([P, PACK * J], F32, "st_all", 4)
        st_sb = [st_all[:, t * J : (t + 1) * J] for t in range(PACK)]
        r_sb = [paged_tile([P, T], F32, "r%d" % t, 4) for t in range(PACK)]

        planes = keep.tile([P, J + N], U8, name="planes", align_bytes=BURST)
        gs = planes[:, 0:J]
        s4_raw = planes[:, J : J + N]
        nc.vector.memset(ts[:].bitcast(I32), 0)
        nc.vector.memset(s4_raw.bitcast(I32), 0)

        r_rows = rT.rearrange("(p t) c -> p t c", t=PACK)
        st_rows = st.rearrange("(p t) j -> p (t j)", t=PACK)

        nc.sync.dma_start(out=wk_raw[:], in_=wk.rearrange("(p i) n -> p i n", i=PACK))
        nc.sync.dma_start(offsets[:], offs)
        staged_rows = slice(0, P, 8)
        nc.sync.dma_start(out=ts[staged_rows, :].bitcast(I32), in_=tab_scales[0].bitcast(I32))
        nc.sync.dma_start(out=planes[staged_rows, J : J + N].bitcast(I32), in_=wv4_scales[0].bitcast(I32))
        nc.sync.dma_start(out=w4_raw[:].bitcast(I32), in_=wv4_words[0].bitcast(I32))
        nc.sync.dma_start(out=tw[:].bitcast(I32), in_=tab_words[0].rearrange("p t i -> p (t i)").bitcast(I32))
        nc.sync.dma_start(out=wd_raw[:], in_=wvd.rearrange("(p i) n -> p i n", i=PACK))

        picked = keep.tile([P, J], U8, name="picked", align_bytes=64)
        nc.vector.tensor_copy(picked[:], ts[:].indirect(offsets[:]))
        nc.vector.tensor_copy(out=gs.bitcast(I32), in_=picked[:].bitcast(I32))
        for r in range(1, 4):
            nc.sync.dma_start(out=planes[r:P:32, :].bitcast(I32), in_=planes[8 * r : P : 32, :].bitcast(I32))

        nc.sync.dma_start(out=st_all[:], in_=st_rows)
        for t in range(PACK):
            nc.sync.dma_start(out=r_sb[t][:], in_=r_rows[:, t, :])

        def round_weight(raw, name, copies):
            grouped = keep.tile([P, PACK, P, PACK], BF16, name=name, align_bytes=64)
            share = P // len(copies)
            for c, copy in enumerate(copies):
                ms = slice(c * share, (c + 1) * share)
                copy(
                    out=grouped[:].rearrange("p t m i -> p m i t")[:, ms],
                    in_=raw[:].rearrange("p i (m t) -> p m i t", t=PACK)[:, ms],
                )
            return grouped

        def quantise_weight(grouped, name):
            codes = keep.tile([P, N], U32, name=name + "_codes", align_bytes=64)
            scales = keep.tile([P, N], U8, name=name + "_scales", align_bytes=64)
            nc.vector.quantize_mx(
                out=codes[:].bitcast(FP8X4), scales=scales[:], in_=grouped[:].rearrange("p t m i -> p (t m i)")
            )
            return codes, scales

        wk_grouped = round_weight(wk_raw, "wk_grouped", [nc.scalar.copy])
        wk_codes, wk_scales = quantise_weight(wk_grouped, "wk")
        w4 = keep.tile([P, 2 * N], U8, name="w4", align_bytes=64)
        nc.vector.tensor_copy(
            out=w4[:].rearrange("p (t m b) -> p t m b", t=PACK, b=2),
            in_=w4_raw[:].rearrange("p (m t b) -> p t m b", t=PACK, b=2),
        )
        gw = [keep.tile([P, HALF], U32, name="gw%d" % h, align_bytes=64) for h in range(2)]
        for h in range(2):
            nc.vector.tensor_copy(gw[h][:], tw[:].indirect(offsets[:, h * HALF // 16 : (h + 1) * HALF // 16]))
        wd_grouped = round_weight(wd_raw, "wd_grouped", [nc.scalar.copy])
        s4 = keep.tile([P, N], U8, name="s4", align_bytes=64)
        nc.vector.tensor_copy(
            out=s4[:].rearrange("p (t m) -> p t m", t=PACK), in_=s4_raw.rearrange("p (m t) -> p t m", t=PACK)
        )
        wd_codes, wd_scales = quantise_weight(wd_grouped, "wd")

        gv = [keep.tile([P, J], F32, name="gv%d" % t) for t in range(PACK)]

        def product(t, h, weights):
            cols = slice(h * HALF, (h + 1) * HALF)
            bank = psum.tile([P, HALF], F32, name="bank")
            for i, (codes, scales) in enumerate(weights):
                nc.tensor.matmul_mx(
                    out=bank[:], lhsT=codes, lhsT_scale=scales, rhs=gw[h][:].bitcast(FP8X4), rhs_scale=gs[:, cols],
                    start=i == 0, stop=i == len(weights) - 1,
                )
            return bank

        def key(t, h):
            ms = slice(t * P, (t + 1) * P)
            return product(t, h, [(wk_codes[:, ms].bitcast(FP8X4), wk_scales[:, ms])])

        def value(t, h):
            ms = slice(t * P, (t + 1) * P)
            base = (w4[:, 2 * t * P : 2 * (t + 1) * P].bitcast(FP4X4), s4[:, ms])
            return product(t, h, [base, (wd_codes[:, ms].bitcast(FP8X4), wd_scales[:, ms])])

        def gate(t, h, ke, engine):
            z = ring.tile([P, HALF], F32, name="z")
            engine.tensor_tensor(z[:], ke[:], st_sb[t][:, h * HALF : (h + 1) * HALF], MULT)
            g = ring.tile([P, HALF], F32, name="g")
            nc.scalar.activation(g[:], z[:], SIGMOID)
            return g

        def let_through(t, h, ve, g):
            nc.vector.tensor_tensor(gv[t][:, h * HALF : (h + 1) * HALF], ve[:], g[:], MULT)

        early = [(t, h) for t in (0, 1) for h in range(2)]
        late = [(t, h) for t in (2, 3) for h in range(2)]
        y_offset = taken[-1]
        keys = {}
        for t, h in late:
            keys[(t, h)] = paged.tile(
                [P, HALF], F32, name="parked%d%d" % (t, h), offset=y_offset + len(keys) * 4 * HALF, align_bytes=BURST
            )
            nc.scalar.copy(out=keys[(t, h)][:], in_=key(t, h)[:])
        for th in early[:-1]:
            keys[th] = key(*th)
        values = {early[0]: value(*early[0])}
        keys[early[-1]] = key(*early[-1])
        values.update({th: value(*th) for th in early[1:]})
        gates = {th: gate(*th, keys[th], nc.vector) for th in early}
        gates.update({th: gate(*th, keys[th], nc.gpsimd) for th in late})
        values.update({th: value(*th) for th in late})
        for th in early + late:
            let_through(*th, values[th], gates[th])

        y = paged_tile([P, PACK * J], F32, "y", 4)
        yb = keep.tile([P, J * PACK], BF16, name="yb", align_bytes=64)
        yb_slots = yb[:].rearrange("p (j t) -> p j t", t=PACK)
        y_codes = paged_tile([P, J], U32, "y_codes", 1)
        y_scales = keep.tile([P, J], U8, name="y_scales", align_bytes=BURST)
        y_rows = out_0.rearrange("(p t) j -> p (t j)", t=PACK)
        word_rows = out_1[0].rearrange("p j i -> p (j i)").bitcast(I32)

        def add_record(t, a, b):
            nc.vector.tensor_tensor(
                y[:, t * J + a : t * J + b], r_sb[t][:].indirect(offsets[:, a // 16 : b // 16]), gv[t][:, a:b], ADD
            )

        def round_slot(t, a, b, copy):
            copy(out=yb_slots[:, a:b, t], in_=y[:, t * J + a : t * J + b])

        def quantise(a, b):
            nc.vector.quantize_mx(
                out=y_codes[:, a:b].bitcast(FP8X4), scales=y_scales[OUT_PLANE:P, a:b], in_=yb[:, PACK * a : PACK * b]
            )

        def store_words(a, b):
            nc.sync.dma_start(out=word_rows[:, a:b], in_=y_codes[:, a:b].bitcast(I32))

        def store_y(a, b):
            nc.sync.dma_start(out=y_rows[:, a:b], in_=y[:, a:b])

        def round_pair(a, b):
            nc.scalar.copy(out=yb_slots[:, a:b, 0:2], in_=y[:, 0 : 2 * J].rearrange("p (e j) -> p j e", e=2)[:, a:b])

        for a in (0, HALF):
            add_record(0, a, a + HALF)
            add_record(1, a, a + HALF)
            round_pair(a, a + HALF)
        add_record(2, 0, HALF)
        add_record(2, HALF, J)
        store_y(0, 2 * J + HALF)
        round_slot(2, 0, HALF, nc.scalar.copy)
        round_slot(2, HALF, J, nc.vector.tensor_copy)

        for a, b in GATHERS:
            add_record(3, a, b)
        for a, b in SCALAR_PIECES:
            round_slot(3, a, b, nc.scalar.copy)
        store_y(2 * J + HALF, 3 * J + HALF)
        store_y(3 * J + HALF, 4 * J)

        quantise(0, 256)
        quantise(256, HALF)
        store_words(0, HALF)
        round_slot(3, *VECTOR_PIECE, nc.vector.tensor_copy)
        quantise(HALF, VECTOR_PIECE[0])
        store_words(HALF, VECTOR_PIECE[0])
        quantise(*VECTOR_PIECE)
        quantise(*SCALAR_PIECES[-1])
        store_words(VECTOR_PIECE[0], J)
        for r in range(4):
            queue = nc.sync if r % 2 == 0 else nc.scalar
            queue.dma_start(
                out=out_2[0, r:16:4, :].bitcast(I32), in_=y_scales[OUT_PLANE + r : P : 32, :].bitcast(I32)
            )
